import numpy as np
import ml_dtypes


def mxq(x, axis, fmt="e4m3"):
    dtype, down = {"e4m3": (ml_dtypes.float8_e4m3fn, 7), "e5m2": (ml_dtypes.float8_e5m2, 14)}[fmt]
    v = np.moveaxis(np.asarray(x, np.float32).astype(ml_dtypes.bfloat16).astype(np.float64), axis, -1)
    blocks = v.reshape(v.shape[:-1] + (-1, 32))
    amax = np.abs(blocks).max(-1, keepdims=True)
    byte = np.maximum(np.where(amax > 0, np.frexp(amax)[1] - 1 + 127, 0) - down, 1)
    scale = np.exp2(byte - 127.0)
    codes = (blocks / scale).astype(np.float32).astype(dtype).astype(np.float64)
    return np.moveaxis((codes * scale).reshape(v.shape), -1, axis)


WIDE = False


def mx_kscale(k):
    if not WIDE:
        return np.ones(k)
    levels = np.array([24, -24, 12, -12, 0])
    if k % 512:
        return np.exp2(np.random.permutation(np.resize(levels, k // 32))).repeat(32)
    a = np.empty((k // 512, 16))
    for p in range(k // 512):
        a[p, :8] = np.random.permutation(np.resize(levels, 8))
        for g in range(8):
            far = levels[np.abs(levels - a[p, g]) >= 10]
            a[p, g + 8] = far[np.random.randint(len(far))]
    return np.exp2(a.ravel()).repeat(32)


def f64(x):
    return np.asarray(x).astype(np.float64)


def striped(idx):
    return np.tile(idx.reshape(-1, 16).T, (8, 1)).astype(np.uint16)


def unstriped(offs):
    return offs[:16].T.reshape(-1).astype(np.int64)


E2M1 = np.array([0.0, 0.5, 1.0, 1.5, 2.0, 3.0, 4.0, 6.0, -0.0, -0.5, -1.0, -1.5, -2.0, -3.0, -4.0, -6.0])


def pack_weight(w, fmt):
    k, n = w.shape
    w = f64(np.asarray(w, np.float32).astype(ml_dtypes.bfloat16)).reshape(k // 32, 32, n)
    amax = np.abs(w).max(1)
    if fmt == "e4m3":
        byte = np.frexp(amax)[1] - 1 + 127 - 7
    else:
        mant, ex = np.frexp(amax / 6.0)
        byte = np.where(mant > 0.5, ex, ex - 1) + 127
    byte = np.clip(np.where(amax > 0, byte, 1), 1, 254)
    scaled = (w * np.exp2(127.0 - byte)[:, None, :]).reshape(k, n).astype(np.float32)
    by_word = np.ascontiguousarray(scaled.reshape(k // 512, 128, 4, n).transpose(0, 1, 3, 2))
    if fmt == "e4m3":
        words = by_word.astype(ml_dtypes.float8_e4m3fn).view(np.uint8)
    else:
        c = by_word.astype(ml_dtypes.float4_e2m1fn).view(np.uint8) & 0xF
        words = (c[..., 0::2] | (c[..., 1::2] << 4)).reshape(k // 512, 128, 2 * n)
    return np.ascontiguousarray(words), np.ascontiguousarray(byte.astype(np.uint8).reshape(k // 512, 16, n))


def unpack_weight(words, scales, fmt):
    g, _, n = scales.shape
    words = np.ascontiguousarray(words).reshape(g, 128, n, -1)
    if fmt == "e4m3":
        vals = words.view(ml_dtypes.float8_e4m3fn).astype(np.float64)
    else:
        nib = np.empty((g, 128, n, 4), np.uint8)
        nib[..., 0::2] = words & 0xF
        nib[..., 1::2] = words >> 4
        vals = E2M1[nib]
    vals = vals * np.repeat(np.exp2(scales.astype(np.float64) - 127.0), 8, axis=1)[..., None]
    return vals.transpose(0, 1, 3, 2).reshape(g * 512, n)


def planes(y):
    n, m = y.shape
    v = y.astype(np.float32).astype(ml_dtypes.bfloat16).astype(np.float64).reshape(n // 32, 32, m)
    top = np.abs(v).max(1)
    byte = np.clip(np.where(top > 0, np.frexp(top)[1] - 1 + 127 - 7, 1), 1, 254)
    codes = (v * np.exp2(127.0 - byte)[:, None, :]).reshape(n, m).astype(np.float32).astype(ml_dtypes.float8_e4m3fn).view(np.uint8)
    words = codes.reshape(n // 512, 128, 4, m).transpose(0, 1, 3, 2)
    return np.ascontiguousarray(words), np.ascontiguousarray(byte.astype(np.uint8).reshape(n // 512, 16, m))


def sigm(f):
    return 1.0 / (1.0 + np.exp(-np.maximum(f, -700.0)))


K, R, N, T, J = 512, 1024, 512, 4096, 1024


def setup_inputs():
    n = np.random.standard_normal
    s = mx_kscale(K)[:, None]
    u = mx_kscale(R)[:, None]
    wd = n((R, N)) / np.sqrt(R) / u
    p_tab = pack_weight(n((K, T)) * s, "e4m3")
    p_wg = pack_weight(n((K, R)) / np.sqrt(K) / s, "e2m1")
    p_wd8 = pack_weight(wd[:512], "e4m3")
    p_wd4 = pack_weight(wd[512:], "e2m1")
    return {
        "tab_words": p_tab[0],
        "tab_scales": p_tab[1],
        "wg_words": p_wg[0],
        "wg_scales": p_wg[1],
        "wu": (n((K, R)) / np.sqrt(K) / s * u.T).astype(np.float32),
        "wd8_words": p_wd8[0],
        "wd8_scales": p_wd8[1],
        "wd4_words": p_wd4[0],
        "wd4_scales": p_wd4[1],
        "rT": (n((N, T))).astype(np.float32),
        "offs": striped(np.random.permutation(T)[:J]),
    }


def reference(tab_words, tab_scales, wg_words, wg_scales, wu, wd8_words, wd8_scales, wd4_words, wd4_scales, rT, offs):
    idx = unstriped(offs)
    tab_ = unpack_weight(tab_words, tab_scales, "e4m3")[:, idx]
    wg_ = unpack_weight(wg_words, wg_scales, "e2m1")
    wu_ = mxq(f64(wu), 0, "e4m3")
    ga = wg_.T @ tab_
    ub = wu_.T @ tab_
    h = sigm(ga) * ub
    h_ = mxq(h, 0, "e4m3")
    wd8_ = unpack_weight(wd8_words, wd8_scales, "e4m3")
    wd4_ = unpack_weight(wd4_words, wd4_scales, "e2m1")
    y = wd8_.T @ h_[:512] + wd4_.T @ h_[512:]
    out_0 = y + f64(rT)[:, idx]
    return (out_0,) + planes(out_0)

@@ -1,0 +1,279 @@
+from contextlib import ExitStack
+
+import concourse.mybir as mybir
+
+K, R, N, T, J = 512, 1024, 512, 4096, 1024
+FLOPS = 2 * K * R * J * 2 + 2 * R * N * J
+
+F32 = mybir.dt.float32
+BF16 = mybir.dt.bfloat16
+I32 = mybir.dt.int32
+U32 = mybir.dt.uint32
+U16 = mybir.dt.uint16
+U8 = mybir.dt.uint8
+E4M3 = mybir.dt.float8_e4m3fn_x4
+E2M1 = mybir.dt.float4_e2m1fn_x4
+ACT = mybir.ActivationFunctionType
+ALU = mybir.AluOpType
+
+P = 128
+PACK = 4
+PASS = P * PACK
+HALF = J // 2
+UNIT = 128
+LIST_COLS = HALF // 16
+
+
+def load_scale_rows(queue, plane, first, rows):
+    for q in range(4):
+        queue.dma_start(
+            out=plane[32 * q + first : 32 * q + first + 4, :].bitcast(I32),
+            in_=rows[4 * q : 4 * q + 4, :].bitcast(I32),
+        )
+
+
+def deal(nc, out, in_):
+    nc.vector.tensor_copy(
+        out=out.rearrange("p (b t m) -> p b t m", t=PACK, m=P),
+        in_=in_.rearrange("p (b m t) -> p b t m", t=PACK, m=P),
+    )
+
+
+def tile_list_gmlpt_sigm_mix_resLP_kernel(
+    tc, tab_words, tab_scales, wg_words, wg_scales, wu, wd8_words, wd8_scales,
+    wd4_words, wd4_scales, rT, offs, out_0, out_1, out_2,
+):
+    nc = tc.nc
+    with ExitStack() as ctx:
+        keep = ctx.enter_context(tc.tile_pool(name="keep", bufs=1))
+        ring = ctx.enter_context(tc.tile_pool(name="ring", bufs=2))
+        psum = ctx.enter_context(tc.psum_pool(name="psum", bufs=1))
+
+        offsets = keep.tile([P, J // 16], U16, name="offsets")
+        tab_w = keep.tile([P, T], I32, name="tab_w", align_bytes=64)
+        tab_s = keep.tile([P, T], U8, name="tab_s", align_bytes=64)
+        wg_w_raw = keep.tile([P, 2 * R], U8, name="wg_w_raw", align_bytes=64)
+        wg_s_raw = keep.tile([P, R], U8, name="wg_s_raw", align_bytes=64)
+        wd8_w_raw = keep.tile([P, N], I32, name="wd8_w_raw", align_bytes=64)
+        wd4_w_raw = keep.tile([P, 2 * N], U8, name="wd4_w_raw", align_bytes=64)
+        wd_s_raw = keep.tile([P, N], U8, name="wd_s_raw", align_bytes=64)
+        warm = keep.tile([P, 8], F32, name="warm")
+        warm_out = keep.tile([P, 8], F32, name="warm_out")
+
+        nc.vector.memset(tab_s[:].bitcast(I32), 0)
+        nc.vector.memset(wg_s_raw[:].bitcast(I32), 0)
+        nc.vector.memset(wd_s_raw[:].bitcast(I32), 0)
+        nc.vector.memset(warm[:], 0.0)
+        nc.scalar.activation(warm_out[:], warm[:], ACT.Sigmoid)
+
+        wu_rows = wu.rearrange("(p i) r -> p i r", i=PACK)
+        wu_cuts = [(0, 256), (256, 512), (512, 768), (768, 1024)]
+        wu_raw = [keep.tile([P, PACK * (c1 - c0)], F32, name="wu_raw%d" % c0) for c0, c1 in wu_cuts]
+
+        def load_wu(piece):
+            c0, c1 = wu_cuts[piece]
+            nc.sync.dma_start(
+                out=wu_raw[piece][:].rearrange("p (i c) -> p i c", i=PACK), in_=wu_rows[:, :, c0:c1]
+            )
+
+        nc.sync.dma_start(offsets[:], offs)
+        nc.sync.dma_start(out=wg_w_raw[:].bitcast(I32), in_=wg_words[0].bitcast(I32))
+        load_wu(0)
+        load_scale_rows(nc.sync, tab_s, 0, tab_scales[0])
+        nc.sync.dma_start(out=tab_w[:], in_=tab_words[0].rearrange("p t i -> p (t i)").bitcast(I32))
+        load_scale_rows(nc.sync, wg_s_raw, 0, wg_scales[0])
+        for piece in range(1, len(wu_cuts)):
+            load_wu(piece)
+
+        r_rows = rT.rearrange("(p t) c -> p t c", t=PACK)
+        r_win = [keep.tile([P, T], F32, name="r_win%d" % t) for t in range(PACK)]
+        nc.sync.dma_start(out=wd8_w_raw[:], in_=wd8_words[0].rearrange("p n i -> p (n i)").bitcast(I32))
+        nc.sync.dma_start(out=wd4_w_raw[:].bitcast(I32), in_=wd4_words[0].bitcast(I32))
+        load_scale_rows(nc.sync, wd_s_raw, 0, wd4_scales[0])
+        nc.sync.dma_start(out=r_win[0][:], in_=r_rows[:, 0, :])
+        load_scale_rows(nc.sync, wd_s_raw, 4, wd8_scales[0])
+        for t in range(1, PACK):
+            nc.sync.dma_start(out=r_win[t][:], in_=r_rows[:, t, :])
+
+        wg_w = keep.tile([P, 2 * R], U8, name="wg_w", align_bytes=64)
+        wg_s = keep.tile([P, R], U8, name="wg_s", align_bytes=64)
+        deal(nc, wg_w[:].bitcast(U16), wg_w_raw[:].bitcast(U16))
+
+        v_s = keep.tile([P, J], U8, name="v_s", align_bytes=64)
+        nc.vector.tensor_copy(v_s[:], tab_s[:].indirect(offsets[:]))
+        lists = [offsets[:, h * LIST_COLS : (h + 1) * LIST_COLS] for h in range(2)]
+        v_w = []
+        for h in range(2):
+            words = keep.tile([P, HALF], U32, name="v_w%d" % h, align_bytes=64)
+            nc.vector.tensor_copy(words[:], tab_w[:].bitcast(U32).indirect(lists[h]))
+            v_w.append(words)
+            if h == 0:
+                deal(nc, wg_s[:], wg_s_raw[:])
+
+        wu_bf = [keep.tile([P, PACK * PASS], BF16, name="wu_bf%d" % b, align_bytes=64) for b in range(2)]
+        wu_w = [keep.tile([P, PASS], U32, name="wu_w%d" % b, align_bytes=64) for b in range(2)]
+        wu_s = [keep.tile([P, PASS], U8, name="wu_s%d" % b, align_bytes=64) for b in range(2)]
+
+        def round_wu(piece, copy):
+            c0, c1 = wu_cuts[piece]
+            b, m0, m1 = c0 // PASS, c0 % PASS // PACK, (c1 - 1) % PASS // PACK + 1
+            copy(
+                out=wu_bf[b][:].rearrange("p (t m i) -> p m t i", t=PACK, i=PACK)[:, m0:m1],
+                in_=wu_raw[piece][:].rearrange("p (i m t) -> p m t i", i=PACK, t=PACK),
+            )
+
+        def quantise_wu(b):
+            nc.vector.quantize_mx(out=wu_w[b][:].bitcast(E4M3), scales=wu_s[b][:], in_=wu_bf[b][:])
+
+        round_wu(0, nc.scalar.copy)
+        round_wu(1, nc.scalar.copy)
+        quantise_wu(0)
+
+        wd8_w = keep.tile([P, N], I32, name="wd8_w", align_bytes=64)
+        wd4_w = keep.tile([P, 2 * N], U8, name="wd4_w", align_bytes=64)
+        wd_s = keep.tile([P, N], U8, name="wd_s", align_bytes=64)
+
+        h_w = {}
+        h_s = {}
+        h_bf = {}
+
+        def gate_and_up(b, u):
+            h, c0 = divmod(u * UNIT, HALF)
+            cols = slice(c0, c0 + UNIT)
+            all_cols = slice(u * UNIT, (u + 1) * UNIT)
+            ga = psum.tile([P, PACK, UNIT], F32, name="ga", bufs=2)
+            for t in range(PACK):
+                w0 = b * PASS + t * P
+                nc.tensor.matmul_mx(
+                    out=ga[:, t, :],
+                    lhsT=wg_w[:, 2 * w0 : 2 * (w0 + P)].bitcast(E2M1),
+                    lhsT_scale=wg_s[:, w0 : w0 + P],
+                    rhs=v_w[h][:, cols].bitcast(E4M3),
+                    rhs_scale=v_s[:, all_cols],
+                    start=True, stop=True,
+                )
+            if b == 0 and u < 2:
+                flat = wu_raw[1][:, u * PASS : (u + 1) * PASS]
+            else:
+                gate_tile = ring.tile([P, UNIT * PACK], F32, name="gate", bufs=8)
+                flat = gate_tile[:]
+            gate = flat.rearrange("p (j t) -> p j t", t=PACK)
+            nc.scalar.activation(gate, ga[:].rearrange("p t j -> p j t"), ACT.Sigmoid)
+            ub = psum.tile([P, PACK, UNIT], F32, name="ub", bufs=3)
+            for t in range(PACK):
+                nc.tensor.matmul_mx(
+                    out=ub[:, t, :],
+                    lhsT=wu_w[b][:, t * P : (t + 1) * P].bitcast(E4M3),
+                    lhsT_scale=wu_s[b][:, t * P : (t + 1) * P],
+                    rhs=v_w[h][:, cols].bitcast(E4M3),
+                    rhs_scale=v_s[:, all_cols],
+                    start=True, stop=True,
+                )
+            if c0 == 0:
+                h_bf[b, h] = ring.tile([P, HALF, PACK], BF16, name="h_bf", align_bytes=64)
+            nc.vector.tensor_tensor(
+                h_bf[b, h][:, cols, :], ub[:].rearrange("p t j -> p j t"), gate, ALU.mult
+            )
+
+        def quantise_h(b, h):
+            h_w[b, h] = keep.tile([P, HALF], U32, name="h_w%d%d" % (b, h), align_bytes=64)
+            h_s[b, h] = keep.tile([P, HALF], U8, name="h_s%d%d" % (b, h), align_bytes=64)
+            nc.vector.quantize_mx(
+                out=h_w[b, h][:].bitcast(E4M3), scales=h_s[b, h][:],
+                in_=h_bf[b, h][:].rearrange("p j t -> p (j t)"),
+            )
+
+        y_sb = {}
+
+        def down(h):
+            for t in range(PACK):
+                y = psum.tile([P, HALF], F32, name="y", bufs=3)
+                nc.tensor.matmul_mx(
+                    out=y[:], lhsT=wd8_w[:, t * P : (t + 1) * P].bitcast(E4M3),
+                    lhsT_scale=wd_s[4:P, t * P : (t + 1) * P],
+                    rhs=h_w[0, h][:].bitcast(E4M3), rhs_scale=h_s[0, h][:],
+                    start=True, stop=False,
+                )
+                nc.tensor.matmul_mx(
+                    out=y[:], lhsT=wd4_w[:, 2 * t * P : 2 * (t + 1) * P].bitcast(E2M1),
+                    lhsT_scale=wd_s[:, t * P : (t + 1) * P],
+                    rhs=h_w[1, h][:].bitcast(E4M3), rhs_scale=h_s[1, h][:],
+                    start=False, stop=True,
+                )
+                y_sb[t, h] = keep.tile([P, HALF], F32, name="y_sb%d%d" % (t, h))
+                nc.scalar.copy(out=y_sb[t, h][:], in_=y[:])
+
+        units = J // UNIT
+        per_half = HALF // UNIT
+        steps = [(b, u) for b in range(2) for u in range(units)]
+        for s, (b, u) in enumerate(steps):
+            gate_and_up(b, u)
+            if s in (3, 5):
+                round_wu(2 + (s - 3) // 2, nc.scalar.copy)
+            if s == 6:
+                quantise_wu(1)
+            if s == 9:
+                deal(nc, wd8_w[:], wd8_w_raw[:])
+                deal(nc, wd4_w[:].bitcast(U16), wd4_w_raw[:].bitcast(U16))
+                deal(nc, wd_s[:], wd_s_raw[:])
+            if s > 0 and s % per_half == 0:
+                pb, pu = steps[s - 1]
+                quantise_h(pb, pu // per_half)
+            if s == 13:
+                down(0)
+        quantise_h(1, 1)
+        down(1)
+
+        out_rows = out_0.rearrange("(p t) j -> p t j", t=PACK)
+        words_out = out_1[0].rearrange("p j i -> p (j i)").bitcast(I32)
+        o_s = keep.tile([P, J], U8, name="o_s", align_bytes=64)
+        chunks = [(0, 512), (512, 768), (768, 1024)]
+        res = [keep.tile([P, PACK, j1 - j0], F32, name="res%d" % j0) for j0, j1 in chunks]
+        res_bf = [keep.tile([P, j1 - j0, PACK], BF16, name="res_bf%d" % j0, align_bytes=64) for j0, j1 in chunks]
+
+        def add_residual(c, t):
+            j0, j1 = chunks[c]
+            h = j0 // HALF
+            nc.vector.tensor_tensor(
+                res[c][:, t, :], r_win[t][:].indirect(offsets[:, j0 // 16 : j1 // 16]),
+                y_sb[t, h][:, j0 - h * HALF : j1 - h * HALF], ALU.add,
+            )
+            nc.sync.dma_start(out=out_rows[:, t, j0:j1], in_=res[c][:, t, :])
+
+        def store_and_round(c, copy):
+            copy(
+                out=res_bf[c][:].rearrange("p (c i) t -> p c t i", i=4),
+                in_=res[c][:].rearrange("p t (c i) -> p c t i", i=4),
+            )
+
+        def quantise_out(c):
+            j0, j1 = chunks[c]
+            o_w = keep.tile([P, j1 - j0], I32, name="o_w%d" % c, align_bytes=64)
+            nc.vector.quantize_mx(
+                out=o_w[:].bitcast(E4M3), scales=o_s[:, j0:j1],
+                in_=res_bf[c][:].rearrange("p j t -> p (j t)"),
+            )
+            nc.sync.dma_start(out=words_out[:, j0:j1], in_=o_w[:])
+
+        for t in range(3):
+            add_residual(0, t)
+        for t in range(2):
+            add_residual(1, t)
+            add_residual(2, t)
+        add_residual(0, 3)
+        store_and_round(0, nc.scalar.copy)
+        add_residual(1, 2)
+        add_residual(1, 3)
+        store_and_round(1, nc.scalar.copy)
+        add_residual(2, 2)
+        add_residual(2, 3)
+        quantise_out(0)
+        store_and_round(2, nc.vector.tensor_copy)
+        quantise_out(1)
+        quantise_out(2)
+        for q in range(4):
+            queue = nc.scalar if q % 2 else nc.sync
+            queue.dma_start(
+                out=out_2[0, 4 * q : 4 * q + 4, :].bitcast(I32),
+                in_=o_s[32 * q : 32 * q + 4, :].bitcast(I32),
+            )

@@ -60,7 +60,8 @@ def tile_list_gmlpt_sigm_mix_resLP_kernel(
         warm = keep.tile([P, 8], F32, name="warm")
         warm_out = keep.tile([P, 8], F32, name="warm_out")
 
-        nc.vector.memset(tab_s[:].bitcast(I32), 0)
+        nc.vector.memset(tab_s[:, : 3 * T // 4].bitcast(I32), 0)
+        nc.gpsimd.memset(tab_s[:, 3 * T // 4 :].bitcast(I32), 0)
         nc.vector.memset(wg_s_raw[:].bitcast(I32), 0)
         nc.vector.memset(wd_s_raw[:].bitcast(I32), 0)
         nc.vector.memset(warm[:], 0.0)
@@ -76,18 +77,17 @@ def tile_list_gmlpt_sigm_mix_resLP_kernel(
                 out=wu_raw[piece][:].rearrange("p (i c) -> p i c", i=PACK), in_=wu_rows[:, :, c0:c1]
             )
 
+        r_rows = rT.rearrange("(p t) c -> p t c", t=PACK)
+        r_win = [keep.tile([P, T], F32, name="r_win%d" % t) for t in range(PACK)]
+
         nc.sync.dma_start(offsets[:], offs)
         nc.sync.dma_start(out=wg_w_raw[:].bitcast(I32), in_=wg_words[0].bitcast(I32))
-        load_wu(0)
+        nc.sync.dma_start(out=wd8_w_raw[:], in_=wd8_words[0].rearrange("p n i -> p (n i)").bitcast(I32))
         load_scale_rows(nc.sync, tab_s, 0, tab_scales[0])
         nc.sync.dma_start(out=tab_w[:], in_=tab_words[0].rearrange("p t i -> p (t i)").bitcast(I32))
         load_scale_rows(nc.sync, wg_s_raw, 0, wg_scales[0])
-        for piece in range(1, len(wu_cuts)):
+        for piece in range(len(wu_cuts)):
             load_wu(piece)
-
-        r_rows = rT.rearrange("(p t) c -> p t c", t=PACK)
-        r_win = [keep.tile([P, T], F32, name="r_win%d" % t) for t in range(PACK)]
-        nc.sync.dma_start(out=wd8_w_raw[:], in_=wd8_words[0].rearrange("p n i -> p (n i)").bitcast(I32))
         nc.sync.dma_start(out=wd4_w_raw[:].bitcast(I32), in_=wd4_words[0].bitcast(I32))
         load_scale_rows(nc.sync, wd_s_raw, 0, wd4_scales[0])
         nc.sync.dma_start(out=r_win[0][:], in_=r_rows[:, 0, :])
@@ -98,6 +98,8 @@ def tile_list_gmlpt_sigm_mix_resLP_kernel(
         wg_w = keep.tile([P, 2 * R], U8, name="wg_w", align_bytes=64)
         wg_s = keep.tile([P, R], U8, name="wg_s", align_bytes=64)
         deal(nc, wg_w[:].bitcast(U16), wg_w_raw[:].bitcast(U16))
+        wd8_w = keep.tile([P, N], I32, name="wd8_w", align_bytes=64)
+        deal(nc, wd8_w[:], wd8_w_raw[:])
 
         v_s = keep.tile([P, J], U8, name="v_s", align_bytes=64)
         nc.vector.tensor_copy(v_s[:], tab_s[:].indirect(offsets[:]))
@@ -129,7 +131,6 @@ def tile_list_gmlpt_sigm_mix_resLP_kernel(
         round_wu(1, nc.scalar.copy)
         quantise_wu(0)
 
-        wd8_w = keep.tile([P, N], I32, name="wd8_w", align_bytes=64)
         wd4_w = keep.tile([P, 2 * N], U8, name="wd4_w", align_bytes=64)
         wd_s = keep.tile([P, N], U8, name="wd_s", align_bytes=64)
 
@@ -152,8 +153,8 @@ def tile_list_gmlpt_sigm_mix_resLP_kernel(
                     rhs_scale=v_s[:, all_cols],
                     start=True, stop=True,
                 )
-            if b == 0 and u < 2:
-                flat = wu_raw[1][:, u * PASS : (u + 1) * PASS]
+            if b == 0 and u % 3 < 2:
+                flat = wu_raw[1 + u // 3][:, u % 3 * PASS : (u % 3 + 1) * PASS]
             else:
                 gate_tile = ring.tile([P, UNIT * PACK], F32, name="gate", bufs=8)
                 flat = gate_tile[:]
@@ -183,94 +184,121 @@ def tile_list_gmlpt_sigm_mix_resLP_kernel(
                 in_=h_bf[b, h][:].rearrange("p j t -> p (j t)"),
             )
 
-        y_sb = {}
+        QUARTER = J // 4
+        res0 = keep.tile([P, PACK, HALF], F32, name="res0")
+        third = keep.tile([P, PACK * QUARTER], F32, name="third")
+        y_first = keep.tile([P, 3, HALF], F32, name="y_first")
+        y_second = keep.tile([P, PACK, HALF], F32, name="y_second")
+        y_sb = {(t, 0): y_first[:, t, :] for t in range(3)}
+        y_sb[3, 0] = third[:, QUARTER : 3 * QUARTER]
+        for t, slot in enumerate((3, 1, 2, 0)):
+            y_sb[t, 1] = y_second[:, slot, :]
 
-        def down(h):
-            for t in range(PACK):
-                y = psum.tile([P, HALF], F32, name="y", bufs=3)
-                nc.tensor.matmul_mx(
-                    out=y[:], lhsT=wd8_w[:, t * P : (t + 1) * P].bitcast(E4M3),
-                    lhsT_scale=wd_s[4:P, t * P : (t + 1) * P],
-                    rhs=h_w[0, h][:].bitcast(E4M3), rhs_scale=h_s[0, h][:],
-                    start=True, stop=False,
-                )
-                nc.tensor.matmul_mx(
-                    out=y[:], lhsT=wd4_w[:, 2 * t * P : 2 * (t + 1) * P].bitcast(E2M1),
-                    lhsT_scale=wd_s[:, t * P : (t + 1) * P],
-                    rhs=h_w[1, h][:].bitcast(E4M3), rhs_scale=h_s[1, h][:],
-                    start=False, stop=True,
-                )
-                y_sb[t, h] = keep.tile([P, HALF], F32, name="y_sb%d%d" % (t, h))
-                nc.scalar.copy(out=y_sb[t, h][:], in_=y[:])
+        def down(t, h):
+            y = psum.tile([P, HALF], F32, name="y", bufs=3)
+            nc.tensor.matmul_mx(
+                out=y[:], lhsT=wd8_w[:, t * P : (t + 1) * P].bitcast(E4M3),
+                lhsT_scale=wd_s[4:P, t * P : (t + 1) * P],
+                rhs=h_w[0, h][:].bitcast(E4M3), rhs_scale=h_s[0, h][:],
+                start=True, stop=False,
+            )
+            nc.tensor.matmul_mx(
+                out=y[:], lhsT=wd4_w[:, 2 * t * P : 2 * (t + 1) * P].bitcast(E2M1),
+                lhsT_scale=wd_s[:, t * P : (t + 1) * P],
+                rhs=h_w[1, h][:].bitcast(E4M3), rhs_scale=h_s[1, h][:],
+                start=False, stop=True,
+            )
+            nc.scalar.copy(out=y_sb[t, h], in_=y[:])
 
         units = J // UNIT
         per_half = HALF // UNIT
         steps = [(b, u) for b in range(2) for u in range(units)]
         for s, (b, u) in enumerate(steps):
             gate_and_up(b, u)
-            if s in (3, 5):
-                round_wu(2 + (s - 3) // 2, nc.scalar.copy)
+            if s in (2, 5):
+                round_wu(2 + s // 3, nc.scalar.copy)
+            if s == 2:
+                deal(nc, wd4_w[:].bitcast(U16), wd4_w_raw[:].bitcast(U16))
             if s == 6:
                 quantise_wu(1)
             if s == 9:
-                deal(nc, wd8_w[:], wd8_w_raw[:])
-                deal(nc, wd4_w[:].bitcast(U16), wd4_w_raw[:].bitcast(U16))
                 deal(nc, wd_s[:], wd_s_raw[:])
             if s > 0 and s % per_half == 0:
                 pb, pu = steps[s - 1]
                 quantise_h(pb, pu // per_half)
-            if s == 13:
-                down(0)
+            if s > 12:
+                down(s - 13, 0)
         quantise_h(1, 1)
-        down(1)
+        down(0, 1)
+        down(3, 0)
+        down(3, 1)
+        down(1, 1)
+        down(2, 1)
 
         out_rows = out_0.rearrange("(p t) j -> p t j", t=PACK)
         words_out = out_1[0].rearrange("p j i -> p (j i)").bitcast(I32)
         o_s = keep.tile([P, J], U8, name="o_s", align_bytes=64)
-        chunks = [(0, 512), (512, 768), (768, 1024)]
-        res = [keep.tile([P, PACK, j1 - j0], F32, name="res%d" % j0) for j0, j1 in chunks]
-        res_bf = [keep.tile([P, j1 - j0, PACK], BF16, name="res_bf%d" % j0, align_bytes=64) for j0, j1 in chunks]
+        homes = [
+            (0, HALF, res0[:]),
+            (HALF, 3 * QUARTER, third[:].rearrange("p (t j) -> p t j", t=PACK)),
+            (3 * QUARTER, J, y_second[:, :, :QUARTER]),
+        ]
 
-        def add_residual(c, t):
-            j0, j1 = chunks[c]
+        def result(j0, j1):
+            first, home = [(a, x) for a, b, x in homes if a <= j0 and j1 <= b][0]
+            return home[:, :, j0 - first : j1 - first]
+
+        def add_residual(t, j0, j1):
             h = j0 // HALF
             nc.vector.tensor_tensor(
-                res[c][:, t, :], r_win[t][:].indirect(offsets[:, j0 // 16 : j1 // 16]),
+                result(j0, j1)[:, t, :], r_win[t][:].indirect(offsets[:, j0 // 16 : j1 // 16]),
                 y_sb[t, h][:, j0 - h * HALF : j1 - h * HALF], ALU.add,
             )
-            nc.sync.dma_start(out=out_rows[:, t, j0:j1], in_=res[c][:, t, :])
 
-        def store_and_round(c, copy):
-            copy(
-                out=res_bf[c][:].rearrange("p (c i) t -> p c t i", i=4),
-                in_=res[c][:].rearrange("p t (c i) -> p c t i", i=4),
+        def store_result(t0, t1, j0, j1):
+            nc.sync.dma_start(out=out_rows[:, t0:t1, j0:j1], in_=result(j0, j1)[:, t0:t1, :])
+
+        res_bf = {}
+        o_w = keep.tile([P, J], I32, name="o_w", align_bytes=64)
+
+        def round_out(j0, j1):
+            res_bf[j0] = keep.tile([P, j1 - j0, PACK], BF16, name="res_bf%d" % j0, align_bytes=64)
+            nc.scalar.copy(
+                out=res_bf[j0][:].rearrange("p (c i) t -> p c t i", i=4),
+                in_=result(j0, j1).rearrange("p t (c i) -> p c t i", i=4),
             )
 
-        def quantise_out(c):
-            j0, j1 = chunks[c]
-            o_w = keep.tile([P, j1 - j0], I32, name="o_w%d" % c, align_bytes=64)
+        def quantise_out(j0, j1):
             nc.vector.quantize_mx(
-                out=o_w[:].bitcast(E4M3), scales=o_s[:, j0:j1],
-                in_=res_bf[c][:].rearrange("p j t -> p (j t)"),
+                out=o_w[:, j0:j1].bitcast(E4M3), scales=o_s[:, j0:j1],
+                in_=res_bf[j0][:].rearrange("p j t -> p (j t)"),
             )
-            nc.sync.dma_start(out=words_out[:, j0:j1], in_=o_w[:])
 
         for t in range(3):
-            add_residual(0, t)
-        for t in range(2):
-            add_residual(1, t)
-            add_residual(2, t)
-        add_residual(0, 3)
-        store_and_round(0, nc.scalar.copy)
-        add_residual(1, 2)
-        add_residual(1, 3)
-        store_and_round(1, nc.scalar.copy)
-        add_residual(2, 2)
-        add_residual(2, 3)
-        quantise_out(0)
-        store_and_round(2, nc.vector.tensor_copy)
-        quantise_out(1)
-        quantise_out(2)
+            add_residual(t, 0, 512)
+            store_result(t, t + 1, 0, 512)
+        add_residual(0, 512, 768)
+        add_residual(3, 0, 512)
+        store_result(3, 4, 0, 512)
+        round_out(0, 512)
+        for t in (3, 1, 2):
+            add_residual(t, 512, 768)
+        store_result(0, 4, 512, 768)
+        round_out(512, 768)
+        for t in range(3):
+            add_residual(t, 768, 1024)
+        store_result(0, 3, 768, 1024)
+        quantise_out(0, 512)
+        nc.sync.dma_start(out=words_out[:, :HALF], in_=o_w[:, :HALF])
+        add_residual(3, 768, 896)
+        round_out(768, 896)
+        add_residual(3, 896, 1024)
+        store_result(3, 4, 768, 1024)
+        round_out(896, 1024)
+        quantise_out(512, 768)
+        quantise_out(768, 896)
+        quantise_out(896, 1024)
+        nc.sync.dma_start(out=words_out[:, HALF:], in_=o_w[:, HALF:])
         for q in range(4):
             queue = nc.scalar if q % 2 else nc.sync
             queue.dma_start(

@@ -25,10 +25,10 @@ LIST_COLS = HALF // 16
 
 
 def load_scale_rows(queue, plane, first, rows):
-    for q in range(4):
+    for r in range(4):
         queue.dma_start(
-            out=plane[32 * q + first : 32 * q + first + 4, :].bitcast(I32),
-            in_=rows[4 * q : 4 * q + 4, :].bitcast(I32),
+            out=plane[first + r : P : 32, :].bitcast(I32),
+            in_=rows[r:16:4, :].bitcast(I32),
         )
 
 
@@ -302,6 +302,6 @@ def tile_list_gmlpt_sigm_mix_resLP_kernel(
         for q in range(4):
             queue = nc.scalar if q % 2 else nc.sync
             queue.dma_start(
-                out=out_2[0, 4 * q : 4 * q + 4, :].bitcast(I32),
-                in_=o_s[32 * q : 32 * q + 4, :].bitcast(I32),
+                out=out_2[0, q:16:4, :].bitcast(I32),
+                in_=o_s[q:P:32, :].bitcast(I32),
             )

@@ -20,6 +20,7 @@ P = 128
 PACK = 4
 PASS = P * PACK
 HALF = J // 2
+QUARTER = J // 4
 UNIT = 128
 LIST_COLS = HALF // 16
 
@@ -36,6 +37,13 @@ def deal(nc, out, in_):
     nc.vector.tensor_copy(
         out=out.rearrange("p (b t m) -> p b t m", t=PACK, m=P),
         in_=in_.rearrange("p (b m t) -> p b t m", t=PACK, m=P),
+    )
+
+
+def deal_words(nc, out, in_):
+    nc.vector.tensor_copy(
+        out=out.rearrange("p (t c i) -> p c t i", t=PACK, i=4),
+        in_=in_.rearrange("p (c i t) -> p c t i", t=PACK, i=4),
     )
 
 
@@ -60,21 +68,20 @@ def tile_list_gmlpt_sigm_mix_resLP_kernel(
         warm = keep.tile([P, 8], F32, name="warm")
         warm_out = keep.tile([P, 8], F32, name="warm_out")
 
-        nc.vector.memset(tab_s[:, : 3 * T // 4].bitcast(I32), 0)
-        nc.gpsimd.memset(tab_s[:, 3 * T // 4 :].bitcast(I32), 0)
+        nc.vector.memset(tab_s[:, : T // 4].bitcast(I32), 0)
+        nc.gpsimd.memset(tab_s[:, T // 4 :].bitcast(I32), 0)
         nc.vector.memset(wg_s_raw[:].bitcast(I32), 0)
-        nc.vector.memset(wd_s_raw[:].bitcast(I32), 0)
         nc.vector.memset(warm[:], 0.0)
+        nc.vector.memset(wd_s_raw[:].bitcast(I32), 0)
         nc.scalar.activation(warm_out[:], warm[:], ACT.Sigmoid)
 
         wu_rows = wu.rearrange("(p i) r -> p i r", i=PACK)
-        wu_cuts = [(0, 256), (256, 512), (512, 768), (768, 1024)]
-        wu_raw = [keep.tile([P, PACK * (c1 - c0)], F32, name="wu_raw%d" % c0) for c0, c1 in wu_cuts]
+        wu_raw = [keep.tile([P, PACK * PASS], F32, name="wu_raw%d" % b) for b in range(2)]
 
-        def load_wu(piece):
-            c0, c1 = wu_cuts[piece]
+        def load_wu(b):
             nc.sync.dma_start(
-                out=wu_raw[piece][:].rearrange("p (i c) -> p i c", i=PACK), in_=wu_rows[:, :, c0:c1]
+                out=wu_raw[b][:].rearrange("p (i c) -> p i c", i=PACK),
+                in_=wu_rows[:, :, b * PASS : (b + 1) * PASS],
             )
 
         r_rows = rT.rearrange("(p t) c -> p t c", t=PACK)
@@ -82,55 +89,60 @@ def tile_list_gmlpt_sigm_mix_resLP_kernel(
 
         nc.sync.dma_start(offsets[:], offs)
         nc.sync.dma_start(out=wg_w_raw[:].bitcast(I32), in_=wg_words[0].bitcast(I32))
-        nc.sync.dma_start(out=wd8_w_raw[:], in_=wd8_words[0].rearrange("p n i -> p (n i)").bitcast(I32))
         load_scale_rows(nc.sync, tab_s, 0, tab_scales[0])
-        nc.sync.dma_start(out=tab_w[:], in_=tab_words[0].rearrange("p t i -> p (t i)").bitcast(I32))
+        load_wu(0)
         load_scale_rows(nc.sync, wg_s_raw, 0, wg_scales[0])
-        for piece in range(len(wu_cuts)):
-            load_wu(piece)
+        nc.sync.dma_start(out=tab_w[:], in_=tab_words[0].rearrange("p t i -> p (t i)").bitcast(I32))
+        load_scale_rows(nc.sync, wd_s_raw, 4, wd8_scales[0])
+        load_wu(1)
+        nc.sync.dma_start(out=wd8_w_raw[:], in_=wd8_words[0].rearrange("p n i -> p (n i)").bitcast(I32))
         nc.sync.dma_start(out=wd4_w_raw[:].bitcast(I32), in_=wd4_words[0].bitcast(I32))
         load_scale_rows(nc.sync, wd_s_raw, 0, wd4_scales[0])
         nc.sync.dma_start(out=r_win[0][:], in_=r_rows[:, 0, :])
-        load_scale_rows(nc.sync, wd_s_raw, 4, wd8_scales[0])
         for t in range(1, PACK):
             nc.sync.dma_start(out=r_win[t][:], in_=r_rows[:, t, :])
 
         wg_w = keep.tile([P, 2 * R], U8, name="wg_w", align_bytes=64)
         wg_s = keep.tile([P, R], U8, name="wg_s", align_bytes=64)
         deal(nc, wg_w[:].bitcast(U16), wg_w_raw[:].bitcast(U16))
-        wd8_w = keep.tile([P, N], I32, name="wd8_w", align_bytes=64)
-        deal(nc, wd8_w[:], wd8_w_raw[:])
 
         v_s = keep.tile([P, J], U8, name="v_s", align_bytes=64)
         nc.vector.tensor_copy(v_s[:], tab_s[:].indirect(offsets[:]))
+        deal(nc, wg_s[:], wg_s_raw[:])
+
+        wu_bf = [keep.tile([P, PACK * PASS], BF16, name="wu_bf%d" % b, align_bytes=64) for b in range(2)]
+        wu_w = [keep.tile([P, PASS], U32, name="wu_w%d" % b, align_bytes=64) for b in range(2)]
+        wu_s = [keep.tile([P, PASS], U8, name="wu_s%d" % b, align_bytes=64) for b in range(2)]
+
+        def round_wu(b, m0, m1):
+            nc.scalar.copy(
+                out=wu_bf[b][:].rearrange("p (t m i) -> p m t i", t=PACK, i=PACK)[:, m0:m1],
+                in_=wu_raw[b][:].rearrange("p (i m t) -> p m t i", i=PACK, t=PACK)[:, m0:m1],
+            )
+
+        def quantise_wu(b):
+            nc.vector.quantize_mx(out=wu_w[b][:].bitcast(E4M3), scales=wu_s[b][:], in_=wu_bf[b][:])
+
+        round_wu(0, 0, P)
+        quantise_wu(0)
+
+        warm_sums = psum.tile([P, HALF], F32, name="ga", bufs=4)
+        for t in range(PACK):
+            nc.tensor.matmul_mx(
+                out=warm_sums[:], lhsT=wg_w[:, 2 * t * P : 2 * (t + 1) * P].bitcast(E2M1),
+                lhsT_scale=wg_s[:, t * P : (t + 1) * P],
+                rhs=wu_w[0][:].bitcast(E4M3), rhs_scale=wu_s[0][:],
+                start=(t == 0), stop=(t == PACK - 1),
+            )
+
         lists = [offsets[:, h * LIST_COLS : (h + 1) * LIST_COLS] for h in range(2)]
         v_w = []
         for h in range(2):
             words = keep.tile([P, HALF], U32, name="v_w%d" % h, align_bytes=64)
             nc.vector.tensor_copy(words[:], tab_w[:].bitcast(U32).indirect(lists[h]))
             v_w.append(words)
-            if h == 0:
-                deal(nc, wg_s[:], wg_s_raw[:])
 
-        wu_bf = [keep.tile([P, PACK * PASS], BF16, name="wu_bf%d" % b, align_bytes=64) for b in range(2)]
-        wu_w = [keep.tile([P, PASS], U32, name="wu_w%d" % b, align_bytes=64) for b in range(2)]
-        wu_s = [keep.tile([P, PASS], U8, name="wu_s%d" % b, align_bytes=64) for b in range(2)]
-
-        def round_wu(piece, copy):
-            c0, c1 = wu_cuts[piece]
-            b, m0, m1 = c0 // PASS, c0 % PASS // PACK, (c1 - 1) % PASS // PACK + 1
-            copy(
-                out=wu_bf[b][:].rearrange("p (t m i) -> p m t i", t=PACK, i=PACK)[:, m0:m1],
-                in_=wu_raw[piece][:].rearrange("p (i m t) -> p m t i", i=PACK, t=PACK),
-            )
-
-        def quantise_wu(b):
-            nc.vector.quantize_mx(out=wu_w[b][:].bitcast(E4M3), scales=wu_s[b][:], in_=wu_bf[b][:])
-
-        round_wu(0, nc.scalar.copy)
-        round_wu(1, nc.scalar.copy)
-        quantise_wu(0)
-
+        wd8_w = keep.tile([P, N], I32, name="wd8_w", align_bytes=64)
         wd4_w = keep.tile([P, 2 * N], U8, name="wd4_w", align_bytes=64)
         wd_s = keep.tile([P, N], U8, name="wd_s", align_bytes=64)
 
@@ -142,7 +154,7 @@ def tile_list_gmlpt_sigm_mix_resLP_kernel(
             h, c0 = divmod(u * UNIT, HALF)
             cols = slice(c0, c0 + UNIT)
             all_cols = slice(u * UNIT, (u + 1) * UNIT)
-            ga = psum.tile([P, PACK, UNIT], F32, name="ga", bufs=2)
+            ga = psum.tile([P, PACK, UNIT], F32, name="ga", bufs=4)
             for t in range(PACK):
                 w0 = b * PASS + t * P
                 nc.tensor.matmul_mx(
@@ -153,14 +165,10 @@ def tile_list_gmlpt_sigm_mix_resLP_kernel(
                     rhs_scale=v_s[:, all_cols],
                     start=True, stop=True,
                 )
-            if b == 0 and u % 3 < 2:
-                flat = wu_raw[1 + u // 3][:, u % 3 * PASS : (u % 3 + 1) * PASS]
-            else:
-                gate_tile = ring.tile([P, UNIT * PACK], F32, name="gate", bufs=8)
-                flat = gate_tile[:]
-            gate = flat.rearrange("p (j t) -> p j t", t=PACK)
+            gate_tile = ring.tile([P, UNIT * PACK], F32, name="gate", bufs=8)
+            gate = gate_tile[:].rearrange("p (j t) -> p j t", t=PACK)
             nc.scalar.activation(gate, ga[:].rearrange("p t j -> p j t"), ACT.Sigmoid)
-            ub = psum.tile([P, PACK, UNIT], F32, name="ub", bufs=3)
+            ub = psum.tile([P, PACK, UNIT], F32, name="ub", bufs=4)
             for t in range(PACK):
                 nc.tensor.matmul_mx(
                     out=ub[:, t, :],
@@ -184,18 +192,18 @@ def tile_list_gmlpt_sigm_mix_resLP_kernel(
                 in_=h_bf[b, h][:].rearrange("p j t -> p (j t)"),
             )
 
-        QUARTER = J // 4
         res0 = keep.tile([P, PACK, HALF], F32, name="res0")
-        third = keep.tile([P, PACK * QUARTER], F32, name="third")
-        y_first = keep.tile([P, 3, HALF], F32, name="y_first")
+        third = keep.tile([P, (PACK + 1) * QUARTER], F32, name="third")
+        y_first = keep.tile([P, 2, HALF], F32, name="y_first")
         y_second = keep.tile([P, PACK, HALF], F32, name="y_second")
-        y_sb = {(t, 0): y_first[:, t, :] for t in range(3)}
-        y_sb[3, 0] = third[:, QUARTER : 3 * QUARTER]
+        y_sb = {(t, 0): y_first[:, t, :] for t in range(2)}
+        y_sb[2, 0] = third[:, : 2 * QUARTER]
+        y_sb[3, 0] = third[:, 2 * QUARTER : 4 * QUARTER]
         for t, slot in enumerate((3, 1, 2, 0)):
             y_sb[t, 1] = y_second[:, slot, :]
 
         def down(t, h):
-            y = psum.tile([P, HALF], F32, name="y", bufs=3)
+            y = psum.tile([P, HALF], F32, name="ga", bufs=4)
             nc.tensor.matmul_mx(
                 out=y[:], lhsT=wd8_w[:, t * P : (t + 1) * P].bitcast(E4M3),
                 lhsT_scale=wd_s[4:P, t * P : (t + 1) * P],
@@ -215,22 +223,23 @@ def tile_list_gmlpt_sigm_mix_resLP_kernel(
         steps = [(b, u) for b in range(2) for u in range(units)]
         for s, (b, u) in enumerate(steps):
             gate_and_up(b, u)
-            if s in (2, 5):
-                round_wu(2 + s // 3, nc.scalar.copy)
+            if 1 <= s <= 4:
+                round_wu(1, (s - 1) * 32, s * 32)
             if s == 2:
-                deal(nc, wd4_w[:].bitcast(U16), wd4_w_raw[:].bitcast(U16))
+                deal_words(nc, wd8_w[:], wd8_w_raw[:])
             if s == 6:
+                deal(nc, wd4_w[:].bitcast(U16), wd4_w_raw[:].bitcast(U16))
+            if s == 5:
                 quantise_wu(1)
             if s == 9:
                 deal(nc, wd_s[:], wd_s_raw[:])
             if s > 0 and s % per_half == 0:
                 pb, pu = steps[s - 1]
                 quantise_h(pb, pu // per_half)
-            if s > 12:
-                down(s - 13, 0)
+        for t in range(PACK):
+            down(t, 0)
         quantise_h(1, 1)
         down(0, 1)
-        down(3, 0)
         down(3, 1)
         down(1, 1)
         down(2, 1)
@@ -240,7 +249,7 @@ def tile_list_gmlpt_sigm_mix_resLP_kernel(
         o_s = keep.tile([P, J], U8, name="o_s", align_bytes=64)
         homes = [
             (0, HALF, res0[:]),
-            (HALF, 3 * QUARTER, third[:].rearrange("p (t j) -> p t j", t=PACK)),
+            (HALF, 3 * QUARTER, third[:, QUARTER:].rearrange("p (t j) -> p t j", t=PACK)),
             (3 * QUARTER, J, y_second[:, :, :QUARTER]),
         ]
 

@@ -148,9 +148,12 @@ def tile_list_gmlpt_sigm_mix_resLP_kernel(
 
         h_w = {}
         h_s = {}
-        h_bf = {}
 
-        def gate_and_up(b, u):
+        h_regions = keep.tile([P, 7 * UNIT * PACK], BF16, name="h_regions", align_bytes=64)
+
+        h_bf = [h_regions[:, 3 * UNIT * PACK * h : 3 * UNIT * PACK * h + PACK * HALF] for h in range(2)]
+
+        def gate_and_up(b, u, on_gpsimd):
             h, c0 = divmod(u * UNIT, HALF)
             cols = slice(c0, c0 + UNIT)
             all_cols = slice(u * UNIT, (u + 1) * UNIT)
@@ -178,29 +181,31 @@ def tile_list_gmlpt_sigm_mix_resLP_kernel(
                     rhs_scale=v_s[:, all_cols],
                     start=True, stop=True,
                 )
-            if c0 == 0:
-                h_bf[b, h] = ring.tile([P, HALF, PACK], BF16, name="h_bf", align_bytes=64)
-            nc.vector.tensor_tensor(
-                h_bf[b, h][:, cols, :], ub[:].rearrange("p t j -> p j t"), gate, ALU.mult
-            )
+            h_unit = h_bf[h][:, PACK * c0 : PACK * (c0 + UNIT)]
+            if on_gpsimd:
+                up_tile = ring.tile([P, UNIT * PACK], F32, name="up")
+                nc.scalar.copy(
+                    out=up_tile[:].rearrange("p (j t) -> p j t", t=PACK), in_=ub[:].rearrange("p t j -> p j t")
+                )
+                nc.gpsimd.tensor_tensor(h_unit, up_tile[:], gate_tile[:], ALU.mult)
+            else:
+                nc.vector.tensor_tensor(
+                    h_unit.rearrange("p (j t) -> p j t", t=PACK), ub[:].rearrange("p t j -> p j t"), gate, ALU.mult
+                )
 
         def quantise_h(b, h):
             h_w[b, h] = keep.tile([P, HALF], U32, name="h_w%d%d" % (b, h), align_bytes=64)
             h_s[b, h] = keep.tile([P, HALF], U8, name="h_s%d%d" % (b, h), align_bytes=64)
             nc.vector.quantize_mx(
                 out=h_w[b, h][:].bitcast(E4M3), scales=h_s[b, h][:],
-                in_=h_bf[b, h][:].rearrange("p j t -> p (j t)"),
+                in_=h_bf[h],
             )
 
         res0 = keep.tile([P, PACK, HALF], F32, name="res0")
-        third = keep.tile([P, (PACK + 1) * QUARTER], F32, name="third")
-        y_first = keep.tile([P, 2, HALF], F32, name="y_first")
-        y_second = keep.tile([P, PACK, HALF], F32, name="y_second")
-        y_sb = {(t, 0): y_first[:, t, :] for t in range(2)}
-        y_sb[2, 0] = third[:, : 2 * QUARTER]
-        y_sb[3, 0] = third[:, 2 * QUARTER : 4 * QUARTER]
-        for t, slot in enumerate((3, 1, 2, 0)):
-            y_sb[t, 1] = y_second[:, slot, :]
+        res1 = keep.tile([P, PACK * HALF], F32, name="res1")
+        y_sb = {(t, h): keep.tile([P, HALF], F32, name="y_sb%d%d" % (t, h))[:] for h in range(2) for t in range(PACK) if h or t < 2}
+        y_sb[2, 0] = res1[:, :HALF]
+        y_sb[3, 0] = res1[:, 2 * HALF : 3 * HALF]
 
         def down(t, h):
             y = psum.tile([P, HALF], F32, name="ga", bufs=4)
@@ -218,39 +223,42 @@ def tile_list_gmlpt_sigm_mix_resLP_kernel(
             )
             nc.scalar.copy(out=y_sb[t, h], in_=y[:])
 
-        units = J // UNIT
-        per_half = HALF // UNIT
-        steps = [(b, u) for b in range(2) for u in range(units)]
-        for s, (b, u) in enumerate(steps):
-            gate_and_up(b, u)
-            if 1 <= s <= 4:
-                round_wu(1, (s - 1) * 32, s * 32)
-            if s == 2:
+        nc.gpsimd.tensor_scalar(
+            wu_bf[1][:].rearrange("p (t m i) -> p m t i", t=PACK, i=PACK),
+            wu_raw[1][:].rearrange("p (i m t) -> p m t i", i=PACK, t=PACK),
+            1.0, 0.0, ALU.mult, ALU.add,
+        )
+        for u in range(4):
+            gate_and_up(0, u, False)
+        for b, h in ((0, 1), (1, 0), (1, 1)):
+            shared = 3 + h
+            own = [u for u in range(4 * h, 4 * h + 4) if u != shared]
+            gate_and_up(b, own[0], False)
+            if (b, h) == (0, 1):
                 deal_words(nc, wd8_w[:], wd8_w_raw[:])
-            if s == 6:
-                deal(nc, wd4_w[:].bitcast(U16), wd4_w_raw[:].bitcast(U16))
-            if s == 5:
                 quantise_wu(1)
-            if s == 9:
+                quantise_h(0, 0)
+            elif (b, h) == (1, 0):
+                deal(nc, wd4_w[:].bitcast(U16), wd4_w_raw[:].bitcast(U16))
                 deal(nc, wd_s[:], wd_s_raw[:])
-            if s > 0 and s % per_half == 0:
-                pb, pu = steps[s - 1]
-                quantise_h(pb, pu // per_half)
+                quantise_h(0, 1)
+            else:
+                quantise_h(1, 0)
+            gate_and_up(b, shared, True)
+            gate_and_up(b, own[1], False)
+            gate_and_up(b, own[2], False)
         for t in range(PACK):
             down(t, 0)
         quantise_h(1, 1)
-        down(0, 1)
-        down(3, 1)
-        down(1, 1)
-        down(2, 1)
+        for t in range(PACK):
+            down(t, 1)
 
         out_rows = out_0.rearrange("(p t) j -> p t j", t=PACK)
         words_out = out_1[0].rearrange("p j i -> p (j i)").bitcast(I32)
         o_s = keep.tile([P, J], U8, name="o_s", align_bytes=64)
         homes = [
             (0, HALF, res0[:]),
-            (HALF, 3 * QUARTER, third[:, QUARTER:].rearrange("p (t j) -> p t j", t=PACK)),
-            (3 * QUARTER, J, y_second[:, :, :QUARTER]),
+            (HALF, J, res1[:].rearrange("p (t j) -> p t j", t=PACK)),
         ]
 
         def result(j0, j1):
@@ -267,47 +275,45 @@ def tile_list_gmlpt_sigm_mix_resLP_kernel(
         def store_result(t0, t1, j0, j1):
             nc.sync.dma_start(out=out_rows[:, t0:t1, j0:j1], in_=result(j0, j1)[:, t0:t1, :])
 
-        res_bf = {}
+        res_bf = keep.tile([P, J * PACK], BF16, name="res_bf", align_bytes=64)
         o_w = keep.tile([P, J], I32, name="o_w", align_bytes=64)
 
-        def round_out(j0, j1):
-            res_bf[j0] = keep.tile([P, j1 - j0, PACK], BF16, name="res_bf%d" % j0, align_bytes=64)
-            nc.scalar.copy(
-                out=res_bf[j0][:].rearrange("p (c i) t -> p c t i", i=4),
+        def round_out(j0, j1, copy):
+            copy(
+                out=res_bf[:, PACK * j0 : PACK * j1].rearrange("p (c i t) -> p c t i", i=4, t=PACK),
                 in_=result(j0, j1).rearrange("p t (c i) -> p c t i", i=4),
             )
 
         def quantise_out(j0, j1):
             nc.vector.quantize_mx(
                 out=o_w[:, j0:j1].bitcast(E4M3), scales=o_s[:, j0:j1],
-                in_=res_bf[j0][:].rearrange("p j t -> p (j t)"),
+                in_=res_bf[:, PACK * j0 : PACK * j1],
             )
 
         for t in range(3):
             add_residual(t, 0, 512)
-            store_result(t, t + 1, 0, 512)
-        add_residual(0, 512, 768)
-        add_residual(3, 0, 512)
+        store_result(0, 3, 0, 512)
+        for t in range(2):
+            add_residual(t, 512, 1024)
+        store_result(0, 2, 512, 1024)
+        add_residual(3, 0, 256)
+        round_out(0, 256, nc.scalar.copy)
+        add_residual(3, 256, 512)
         store_result(3, 4, 0, 512)
-        round_out(0, 512)
-        for t in (3, 1, 2):
-            add_residual(t, 512, 768)
-        store_result(0, 4, 512, 768)
-        round_out(512, 768)
-        for t in range(3):
-            add_residual(t, 768, 1024)
-        store_result(0, 3, 768, 1024)
+        round_out(256, 512, nc.scalar.copy)
+        for j0 in (512, 768):
+            add_residual(2, j0, j0 + 256)
+            add_residual(3, j0, j0 + 256)
+            store_result(2, 4, j0, j0 + 256)
+        round_out(512, 768, nc.scalar.copy)
+        round_out(768, 896, nc.scalar.copy)
         quantise_out(0, 512)
         nc.sync.dma_start(out=words_out[:, :HALF], in_=o_w[:, :HALF])
-        add_residual(3, 768, 896)
-        round_out(768, 896)
-        add_residual(3, 896, 1024)
-        store_result(3, 4, 768, 1024)
-        round_out(896, 1024)
+        round_out(896, 1024, nc.vector.tensor_copy)
         quantise_out(512, 768)
-        quantise_out(768, 896)
-        quantise_out(896, 1024)
-        nc.sync.dma_start(out=words_out[:, HALF:], in_=o_w[:, HALF:])
+        nc.sync.dma_start(out=words_out[:, 512:768], in_=o_w[:, 512:768])
+        quantise_out(768, 1024)
+        nc.sync.dma_start(out=words_out[:, 768:], in_=o_w[:, 768:])
         for q in range(4):
             queue = nc.scalar if q % 2 else nc.sync
             queue.dma_start(

@@ -23,6 +23,8 @@ HALF = J // 2
 QUARTER = J // 4
 UNIT = 128
 LIST_COLS = HALF // 16
+STAGE = P - 16
+LAST = J - J // 8
 
 
 def load_scale_rows(queue, plane, first, rows):
@@ -64,7 +66,7 @@ def tile_list_gmlpt_sigm_mix_resLP_kernel(
         wg_s_raw = keep.tile([P, R], U8, name="wg_s_raw", align_bytes=64)
         wd8_w_raw = keep.tile([P, N], I32, name="wd8_w_raw", align_bytes=64)
         wd4_w_raw = keep.tile([P, 2 * N], U8, name="wd4_w_raw", align_bytes=64)
-        wd_s_raw = keep.tile([P, N], U8, name="wd_s_raw", align_bytes=64)
+        wd_s_raw = keep.tile([P, 2 * N], U8, name="wd_s_raw", align_bytes=64)
         warm = keep.tile([P, 8], F32, name="warm")
         warm_out = keep.tile([P, 8], F32, name="warm_out")
 
@@ -72,11 +74,11 @@ def tile_list_gmlpt_sigm_mix_resLP_kernel(
         nc.gpsimd.memset(tab_s[:, T // 4 :].bitcast(I32), 0)
         nc.vector.memset(wg_s_raw[:].bitcast(I32), 0)
         nc.vector.memset(warm[:], 0.0)
-        nc.vector.memset(wd_s_raw[:].bitcast(I32), 0)
+        nc.vector.memset(wd_s_raw[:STAGE, :].bitcast(I32), 0)
         nc.scalar.activation(warm_out[:], warm[:], ACT.Sigmoid)
 
         wu_rows = wu.rearrange("(p i) r -> p i r", i=PACK)
-        wu_raw = [keep.tile([P, PACK * PASS], F32, name="wu_raw%d" % b) for b in range(2)]
+        wu_raw = [keep.tile([P, PACK * PASS], F32, name="wu_raw%d" % b, align_bytes=64) for b in range(2)]
 
         def load_wu(b):
             nc.sync.dma_start(
@@ -91,16 +93,14 @@ def tile_list_gmlpt_sigm_mix_resLP_kernel(
         nc.sync.dma_start(out=wg_w_raw[:].bitcast(I32), in_=wg_words[0].bitcast(I32))
         load_scale_rows(nc.sync, tab_s, 0, tab_scales[0])
         load_wu(0)
+        nc.sync.dma_start(out=wd_s_raw[STAGE:, :N].bitcast(I32), in_=wd8_scales[0].bitcast(I32))
+        nc.sync.dma_start(out=wd_s_raw[STAGE:, N:].bitcast(I32), in_=wd4_scales[0].bitcast(I32))
         load_scale_rows(nc.sync, wg_s_raw, 0, wg_scales[0])
         nc.sync.dma_start(out=tab_w[:], in_=tab_words[0].rearrange("p t i -> p (t i)").bitcast(I32))
-        load_scale_rows(nc.sync, wd_s_raw, 4, wd8_scales[0])
         load_wu(1)
         nc.sync.dma_start(out=wd8_w_raw[:], in_=wd8_words[0].rearrange("p n i -> p (n i)").bitcast(I32))
         nc.sync.dma_start(out=wd4_w_raw[:].bitcast(I32), in_=wd4_words[0].bitcast(I32))
-        load_scale_rows(nc.sync, wd_s_raw, 0, wd4_scales[0])
         nc.sync.dma_start(out=r_win[0][:], in_=r_rows[:, 0, :])
-        for t in range(1, PACK):
-            nc.sync.dma_start(out=r_win[t][:], in_=r_rows[:, t, :])
 
         wg_w = keep.tile([P, 2 * R], U8, name="wg_w", align_bytes=64)
         wg_s = keep.tile([P, R], U8, name="wg_s", align_bytes=64)
@@ -109,6 +109,14 @@ def tile_list_gmlpt_sigm_mix_resLP_kernel(
         v_s = keep.tile([P, J], U8, name="v_s", align_bytes=64)
         nc.vector.tensor_copy(v_s[:], tab_s[:].indirect(offsets[:]))
         deal(nc, wg_s[:], wg_s_raw[:])
+        wd_s = keep.tile([P, 2 * N], U8, name="wd_s", align_bytes=64)
+        deal(nc, wd_s[:], wd_s_raw[:])
+        for r in range(4):
+            nc.sync.dma_start(
+                out=wd_s[r:P:32, :].bitcast(I32), in_=wd_s[STAGE + r : P : 4, :].bitcast(I32)
+            )
+        for t in range(1, PACK):
+            nc.sync.dma_start(out=r_win[t][:], in_=r_rows[:, t, :])
 
         wu_bf = [keep.tile([P, PACK * PASS], BF16, name="wu_bf%d" % b, align_bytes=64) for b in range(2)]
         wu_w = [keep.tile([P, PASS], U32, name="wu_w%d" % b, align_bytes=64) for b in range(2)]
@@ -142,9 +150,7 @@ def tile_list_gmlpt_sigm_mix_resLP_kernel(
             nc.vector.tensor_copy(words[:], tab_w[:].bitcast(U32).indirect(lists[h]))
             v_w.append(words)
 
-        wd8_w = keep.tile([P, N], I32, name="wd8_w", align_bytes=64)
         wd4_w = keep.tile([P, 2 * N], U8, name="wd4_w", align_bytes=64)
-        wd_s = keep.tile([P, N], U8, name="wd_s", align_bytes=64)
 
         h_w = {}
         h_s = {}
@@ -201,23 +207,25 @@ def tile_list_gmlpt_sigm_mix_resLP_kernel(
                 in_=h_bf[h],
             )
 
-        res0 = keep.tile([P, PACK, HALF], F32, name="res0")
-        res1 = keep.tile([P, PACK * HALF], F32, name="res1")
-        y_sb = {(t, h): keep.tile([P, HALF], F32, name="y_sb%d%d" % (t, h))[:] for h in range(2) for t in range(PACK) if h or t < 2}
-        y_sb[2, 0] = res1[:, :HALF]
-        y_sb[3, 0] = res1[:, 2 * HALF : 3 * HALF]
+        res_flat = keep.tile([P, PACK * J], F32, name="res")
+        res = res_flat[:].rearrange("p (t j) -> p t j", t=PACK)
+        y_sb = {
+            (t, h): keep.tile([P, HALF], F32, name="y_sb%d%d" % (t, h), align_bytes=64)[:]
+            for h in range(2) for t in range(PACK) if (t, h) != (1, 0)
+        }
+        y_sb[1, 0] = res_flat[:, HALF:J]
 
         def down(t, h):
             y = psum.tile([P, HALF], F32, name="ga", bufs=4)
             nc.tensor.matmul_mx(
                 out=y[:], lhsT=wd8_w[:, t * P : (t + 1) * P].bitcast(E4M3),
-                lhsT_scale=wd_s[4:P, t * P : (t + 1) * P],
+                lhsT_scale=wd_s[:, t * P : (t + 1) * P],
                 rhs=h_w[0, h][:].bitcast(E4M3), rhs_scale=h_s[0, h][:],
                 start=True, stop=False,
             )
             nc.tensor.matmul_mx(
                 out=y[:], lhsT=wd4_w[:, 2 * t * P : 2 * (t + 1) * P].bitcast(E2M1),
-                lhsT_scale=wd_s[:, t * P : (t + 1) * P],
+                lhsT_scale=wd_s[:, N + t * P : N + (t + 1) * P],
                 rhs=h_w[1, h][:].bitcast(E4M3), rhs_scale=h_s[1, h][:],
                 start=False, stop=True,
             )
@@ -228,6 +236,7 @@ def tile_list_gmlpt_sigm_mix_resLP_kernel(
             wu_raw[1][:].rearrange("p (i m t) -> p m t i", i=PACK, t=PACK),
             1.0, 0.0, ALU.mult, ALU.add,
         )
+        wd8_w = keep.tile([P, N], I32, name="wu_raw1", align_bytes=64)
         for u in range(4):
             gate_and_up(0, u, False)
         for b, h in ((0, 1), (1, 0), (1, 1)):
@@ -240,7 +249,6 @@ def tile_list_gmlpt_sigm_mix_resLP_kernel(
                 quantise_h(0, 0)
             elif (b, h) == (1, 0):
                 deal(nc, wd4_w[:].bitcast(U16), wd4_w_raw[:].bitcast(U16))
-                deal(nc, wd_s[:], wd_s_raw[:])
                 quantise_h(0, 1)
             else:
                 quantise_h(1, 0)
@@ -256,64 +264,57 @@ def tile_list_gmlpt_sigm_mix_resLP_kernel(
         out_rows = out_0.rearrange("(p t) j -> p t j", t=PACK)
         words_out = out_1[0].rearrange("p j i -> p (j i)").bitcast(I32)
         o_s = keep.tile([P, J], U8, name="o_s", align_bytes=64)
-        homes = [
-            (0, HALF, res0[:]),
-            (HALF, J, res1[:].rearrange("p (t j) -> p t j", t=PACK)),
-        ]
-
-        def result(j0, j1):
-            first, home = [(a, x) for a, b, x in homes if a <= j0 and j1 <= b][0]
-            return home[:, :, j0 - first : j1 - first]
-
         def add_residual(t, j0, j1):
             h = j0 // HALF
             nc.vector.tensor_tensor(
-                result(j0, j1)[:, t, :], r_win[t][:].indirect(offsets[:, j0 // 16 : j1 // 16]),
+                res[:, t, j0:j1], r_win[t][:].indirect(offsets[:, j0 // 16 : j1 // 16]),
                 y_sb[t, h][:, j0 - h * HALF : j1 - h * HALF], ALU.add,
             )
 
         def store_result(t0, t1, j0, j1):
-            nc.sync.dma_start(out=out_rows[:, t0:t1, j0:j1], in_=result(j0, j1)[:, t0:t1, :])
+            nc.sync.dma_start(out=out_rows[:, t0:t1, j0:j1], in_=res[:, t0:t1, j0:j1])
 
-        res_bf = keep.tile([P, J * PACK], BF16, name="res_bf", align_bytes=64)
+        res_bf = {}
         o_w = keep.tile([P, J], I32, name="o_w", align_bytes=64)
 
-        def round_out(j0, j1, copy):
+        def rounded(j0, j1):
+            h = j0 // HALF
+            return res_bf[h][:, PACK * (j0 - h * HALF) : PACK * (j1 - h * HALF)]
+
+        def round_pair(t0, j0, j1, copy):
             copy(
-                out=res_bf[:, PACK * j0 : PACK * j1].rearrange("p (c i t) -> p c t i", i=4, t=PACK),
-                in_=result(j0, j1).rearrange("p t (c i) -> p c t i", i=4),
+                out=rounded(j0, j1).rearrange("p (c i t) -> p c t i", i=2, t=PACK)[:, :, t0 : t0 + 2],
+                in_=res[:, t0 : t0 + 2, j0:j1].rearrange("p t (c i) -> p c t i", i=2),
             )
 
         def quantise_out(j0, j1):
             nc.vector.quantize_mx(
                 out=o_w[:, j0:j1].bitcast(E4M3), scales=o_s[:, j0:j1],
-                in_=res_bf[:, PACK * j0 : PACK * j1],
+                in_=rounded(j0, j1),
             )
 
-        for t in range(3):
-            add_residual(t, 0, 512)
-        store_result(0, 3, 0, 512)
         for t in range(2):
-            add_residual(t, 512, 1024)
-        store_result(0, 2, 512, 1024)
-        add_residual(3, 0, 256)
-        round_out(0, 256, nc.scalar.copy)
-        add_residual(3, 256, 512)
-        store_result(3, 4, 0, 512)
-        round_out(256, 512, nc.scalar.copy)
-        for j0 in (512, 768):
-            add_residual(2, j0, j0 + 256)
-            add_residual(3, j0, j0 + 256)
-            store_result(2, 4, j0, j0 + 256)
-        round_out(512, 768, nc.scalar.copy)
-        round_out(768, 896, nc.scalar.copy)
-        quantise_out(0, 512)
-        nc.sync.dma_start(out=words_out[:, :HALF], in_=o_w[:, :HALF])
-        round_out(896, 1024, nc.vector.tensor_copy)
-        quantise_out(512, 768)
-        nc.sync.dma_start(out=words_out[:, 512:768], in_=o_w[:, 512:768])
-        quantise_out(768, 1024)
-        nc.sync.dma_start(out=words_out[:, 768:], in_=o_w[:, 768:])
+            add_residual(t, 0, HALF)
+        add_residual(0, HALF, J)
+        res_bf[0] = keep.tile([P, HALF * PACK], BF16, name="y_sb01", align_bytes=64)
+        res_bf[1] = keep.tile([P, HALF * PACK], BF16, name="res_bf1", align_bytes=64)
+        round_pair(0, 0, HALF, nc.scalar.copy)
+        add_residual(1, HALF, J)
+        round_pair(0, HALF, J, nc.scalar.copy)
+        store_result(0, 2, 0, J)
+        add_residual(2, 0, HALF)
+        add_residual(2, HALF, J)
+        store_result(2, 3, 0, J)
+        for j0 in range(0, J, QUARTER):
+            add_residual(3, j0, j0 + QUARTER)
+            round_pair(2, j0, min(j0 + QUARTER, LAST), nc.scalar.copy)
+            if j0 % HALF:
+                store_result(3, 4, j0 - QUARTER, j0 + QUARTER)
+        for j0, j1 in ((0, 512), (512, 768), (768, 1024)):
+            quantise_out(j0, j1)
+            if j0 == 0:
+                round_pair(2, LAST, J, nc.vector.tensor_copy)
+            nc.sync.dma_start(out=words_out[:, j0:j1], in_=o_w[:, j0:j1])
         for q in range(4):
             queue = nc.scalar if q % 2 else nc.sync
             queue.dma_start(

@@ -70,9 +70,10 @@ def tile_list_gmlpt_sigm_mix_resLP_kernel(
         warm = keep.tile([P, 8], F32, name="warm")
         warm_out = keep.tile([P, 8], F32, name="warm_out")
 
-        nc.vector.memset(tab_s[:, : T // 4].bitcast(I32), 0)
-        nc.gpsimd.memset(tab_s[:, T // 4 :].bitcast(I32), 0)
+        v_s = keep.tile([P, J], U8, name="v_s", align_bytes=64)
         nc.vector.memset(wg_s_raw[:].bitcast(I32), 0)
+        nc.vector.memset(tab_s[:STAGE, :].bitcast(I32), 0)
+        nc.vector.memset(v_s[:].bitcast(I32), 0)
         nc.vector.memset(warm[:], 0.0)
         nc.vector.memset(wd_s_raw[:STAGE, :].bitcast(I32), 0)
         nc.scalar.activation(warm_out[:], warm[:], ACT.Sigmoid)
@@ -90,13 +91,19 @@ def tile_list_gmlpt_sigm_mix_resLP_kernel(
         r_win = [keep.tile([P, T], F32, name="r_win%d" % t) for t in range(PACK)]
 
         nc.sync.dma_start(offsets[:], offs)
+        nc.sync.dma_start(out=tab_s[STAGE:, :].bitcast(I32), in_=tab_scales[0].bitcast(I32))
         nc.sync.dma_start(out=wg_w_raw[:].bitcast(I32), in_=wg_words[0].bitcast(I32))
-        load_scale_rows(nc.sync, tab_s, 0, tab_scales[0])
         load_wu(0)
         nc.sync.dma_start(out=wd_s_raw[STAGE:, :N].bitcast(I32), in_=wd8_scales[0].bitcast(I32))
         nc.sync.dma_start(out=wd_s_raw[STAGE:, N:].bitcast(I32), in_=wd4_scales[0].bitcast(I32))
         load_scale_rows(nc.sync, wg_s_raw, 0, wg_scales[0])
         nc.sync.dma_start(out=tab_w[:], in_=tab_words[0].rearrange("p t i -> p (t i)").bitcast(I32))
+        v_s_staged = keep.tile([P, J], U8, name="v_s_staged", align_bytes=64)
+        nc.vector.tensor_copy(v_s_staged[:], tab_s[:].indirect(offsets[:]))
+        for r in range(4):
+            nc.sync.dma_start(
+                out=v_s[r:P:32, :].bitcast(I32), in_=v_s_staged[STAGE + r : P : 4, :].bitcast(I32)
+            )
         load_wu(1)
         nc.sync.dma_start(out=wd8_w_raw[:], in_=wd8_words[0].rearrange("p n i -> p (n i)").bitcast(I32))
         nc.sync.dma_start(out=wd4_w_raw[:].bitcast(I32), in_=wd4_words[0].bitcast(I32))
@@ -106,8 +113,6 @@ def tile_list_gmlpt_sigm_mix_resLP_kernel(
         wg_s = keep.tile([P, R], U8, name="wg_s", align_bytes=64)
         deal(nc, wg_w[:].bitcast(U16), wg_w_raw[:].bitcast(U16))
 
-        v_s = keep.tile([P, J], U8, name="v_s", align_bytes=64)
-        nc.vector.tensor_copy(v_s[:], tab_s[:].indirect(offsets[:]))
         deal(nc, wg_s[:], wg_s_raw[:])
         wd_s = keep.tile([P, 2 * N], U8, name="wd_s", align_bytes=64)
         deal(nc, wd_s[:], wd_s_raw[:])

@@ -27,14 +27,6 @@ STAGE = P - 16
 LAST = J - J // 8
 
 
-def load_scale_rows(queue, plane, first, rows):
-    for r in range(4):
-        queue.dma_start(
-            out=plane[first + r : P : 32, :].bitcast(I32),
-            in_=rows[r:16:4, :].bitcast(I32),
-        )
-
-
 def deal(nc, out, in_):
     nc.vector.tensor_copy(
         out=out.rearrange("p (b t m) -> p b t m", t=PACK, m=P),
@@ -63,19 +55,15 @@ def tile_list_gmlpt_sigm_mix_resLP_kernel(
         tab_w = keep.tile([P, T], I32, name="tab_w", align_bytes=64)
         tab_s = keep.tile([P, T], U8, name="tab_s", align_bytes=64)
         wg_w_raw = keep.tile([P, 2 * R], U8, name="wg_w_raw", align_bytes=64)
-        wg_s_raw = keep.tile([P, R], U8, name="wg_s_raw", align_bytes=64)
         wd8_w_raw = keep.tile([P, N], I32, name="wd8_w_raw", align_bytes=64)
         wd4_w_raw = keep.tile([P, 2 * N], U8, name="wd4_w_raw", align_bytes=64)
-        wd_s_raw = keep.tile([P, 2 * N], U8, name="wd_s_raw", align_bytes=64)
+        w_s_raw = keep.tile([P, R + 2 * N], U8, name="w_s_raw", align_bytes=64)
         warm = keep.tile([P, 8], F32, name="warm")
         warm_out = keep.tile([P, 8], F32, name="warm_out")
 
-        v_s = keep.tile([P, J], U8, name="v_s", align_bytes=64)
-        nc.vector.memset(wg_s_raw[:].bitcast(I32), 0)
-        nc.vector.memset(tab_s[:STAGE, :].bitcast(I32), 0)
-        nc.vector.memset(v_s[:].bitcast(I32), 0)
         nc.vector.memset(warm[:], 0.0)
-        nc.vector.memset(wd_s_raw[:STAGE, :].bitcast(I32), 0)
+        nc.vector.memset(tab_s[:STAGE, :].bitcast(I32), 0)
+        nc.vector.memset(w_s_raw[:STAGE, :].bitcast(I32), 0)
         nc.scalar.activation(warm_out[:], warm[:], ACT.Sigmoid)
 
         wu_rows = wu.rearrange("(p i) r -> p i r", i=PACK)
@@ -92,17 +80,22 @@ def tile_list_gmlpt_sigm_mix_resLP_kernel(
 
         nc.sync.dma_start(offsets[:], offs)
         nc.sync.dma_start(out=tab_s[STAGE:, :].bitcast(I32), in_=tab_scales[0].bitcast(I32))
+        nc.sync.dma_start(out=w_s_raw[STAGE:, :R].bitcast(I32), in_=wg_scales[0].bitcast(I32))
         nc.sync.dma_start(out=wg_w_raw[:].bitcast(I32), in_=wg_words[0].bitcast(I32))
         load_wu(0)
-        nc.sync.dma_start(out=wd_s_raw[STAGE:, :N].bitcast(I32), in_=wd8_scales[0].bitcast(I32))
-        nc.sync.dma_start(out=wd_s_raw[STAGE:, N:].bitcast(I32), in_=wd4_scales[0].bitcast(I32))
-        load_scale_rows(nc.sync, wg_s_raw, 0, wg_scales[0])
+        nc.sync.dma_start(out=w_s_raw[STAGE:, R : R + N].bitcast(I32), in_=wd8_scales[0].bitcast(I32))
+        nc.sync.dma_start(out=w_s_raw[STAGE:, R + N :].bitcast(I32), in_=wd4_scales[0].bitcast(I32))
         nc.sync.dma_start(out=tab_w[:], in_=tab_words[0].rearrange("p t i -> p (t i)").bitcast(I32))
         v_s_staged = keep.tile([P, J], U8, name="v_s_staged", align_bytes=64)
         nc.vector.tensor_copy(v_s_staged[:], tab_s[:].indirect(offsets[:]))
+        first_s = keep.tile([P, R + J], U8, name="first_s", align_bytes=64)
+        wg_s = first_s[:, :R]
+        v_s = first_s[:, R:]
+        deal(nc, wg_s, w_s_raw[:, :R])
+        nc.vector.tensor_copy(v_s.bitcast(I32), v_s_staged[:].bitcast(I32))
         for r in range(4):
             nc.sync.dma_start(
-                out=v_s[r:P:32, :].bitcast(I32), in_=v_s_staged[STAGE + r : P : 4, :].bitcast(I32)
+                out=first_s[r:P:32, :].bitcast(I32), in_=first_s[STAGE + r : P : 4, :].bitcast(I32)
             )
         load_wu(1)
         nc.sync.dma_start(out=wd8_w_raw[:], in_=wd8_words[0].rearrange("p n i -> p (n i)").bitcast(I32))
@@ -110,12 +103,10 @@ def tile_list_gmlpt_sigm_mix_resLP_kernel(
         nc.sync.dma_start(out=r_win[0][:], in_=r_rows[:, 0, :])
 
         wg_w = keep.tile([P, 2 * R], U8, name="wg_w", align_bytes=64)
-        wg_s = keep.tile([P, R], U8, name="wg_s", align_bytes=64)
         deal(nc, wg_w[:].bitcast(U16), wg_w_raw[:].bitcast(U16))
 
-        deal(nc, wg_s[:], wg_s_raw[:])
         wd_s = keep.tile([P, 2 * N], U8, name="wd_s", align_bytes=64)
-        deal(nc, wd_s[:], wd_s_raw[:])
+        deal(nc, wd_s[:], w_s_raw[:, R:])
         for r in range(4):
             nc.sync.dma_start(
                 out=wd_s[r:P:32, :].bitcast(I32), in_=wd_s[STAGE + r : P : 4, :].bitcast(I32)
@@ -142,8 +133,8 @@ def tile_list_gmlpt_sigm_mix_resLP_kernel(
         warm_sums = psum.tile([P, HALF], F32, name="ga", bufs=4)
         for t in range(PACK):
             nc.tensor.matmul_mx(
-                out=warm_sums[:], lhsT=wg_w[:, 2 * t * P : 2 * (t + 1) * P].bitcast(E2M1),
-                lhsT_scale=wg_s[:, t * P : (t + 1) * P],
+                out=warm_sums[:], lhsT=wu_w[0][:, t * P : (t + 1) * P].bitcast(E4M3),
+                lhsT_scale=wu_s[0][:, t * P : (t + 1) * P],
                 rhs=wu_w[0][:].bitcast(E4M3), rhs_scale=wu_s[0][:],
                 start=(t == 0), stop=(t == PACK - 1),
             )

@@ -88,11 +88,13 @@ def tile_list_gmlpt_sigm_mix_resLP_kernel(
         nc.sync.dma_start(out=tab_w[:], in_=tab_words[0].rearrange("p t i -> p (t i)").bitcast(I32))
         v_s_staged = keep.tile([P, J], U8, name="v_s_staged", align_bytes=64)
         nc.vector.tensor_copy(v_s_staged[:], tab_s[:].indirect(offsets[:]))
-        first_s = keep.tile([P, R + J], U8, name="first_s", align_bytes=64)
+        first_s = keep.tile([P, R + J + 2 * N], U8, name="first_s", align_bytes=64)
         wg_s = first_s[:, :R]
-        v_s = first_s[:, R:]
+        v_s = first_s[:, R : R + J]
+        wd_s = first_s[:, R + J :]
         deal(nc, wg_s, w_s_raw[:, :R])
         nc.vector.tensor_copy(v_s.bitcast(I32), v_s_staged[:].bitcast(I32))
+        deal(nc, wd_s, w_s_raw[:, R:])
         for r in range(4):
             nc.sync.dma_start(
                 out=first_s[r:P:32, :].bitcast(I32), in_=first_s[STAGE + r : P : 4, :].bitcast(I32)
@@ -105,12 +107,6 @@ def tile_list_gmlpt_sigm_mix_resLP_kernel(
         wg_w = keep.tile([P, 2 * R], U8, name="wg_w", align_bytes=64)
         deal(nc, wg_w[:].bitcast(U16), wg_w_raw[:].bitcast(U16))
 
-        wd_s = keep.tile([P, 2 * N], U8, name="wd_s", align_bytes=64)
-        deal(nc, wd_s[:], w_s_raw[:, R:])
-        for r in range(4):
-            nc.sync.dma_start(
-                out=wd_s[r:P:32, :].bitcast(I32), in_=wd_s[STAGE + r : P : 4, :].bitcast(I32)
-            )
         for t in range(1, PACK):
             nc.sync.dma_start(out=r_win[t][:], in_=r_rows[:, t, :])
 

@@ -22,7 +22,6 @@ PASS = P * PACK
 HALF = J // 2
 QUARTER = J // 4
 UNIT = 128
-LIST_COLS = HALF // 16
 STAGE = P - 16
 LAST = J - J // 8
 
@@ -114,8 +113,8 @@ def tile_list_gmlpt_sigm_mix_resLP_kernel(
         wu_w = [keep.tile([P, PASS], U32, name="wu_w%d" % b, align_bytes=64) for b in range(2)]
         wu_s = [keep.tile([P, PASS], U8, name="wu_s%d" % b, align_bytes=64) for b in range(2)]
 
-        def round_wu(b, m0, m1):
-            nc.scalar.copy(
+        def round_wu(b, m0, m1, copy):
+            copy(
                 out=wu_bf[b][:].rearrange("p (t m i) -> p m t i", t=PACK, i=PACK)[:, m0:m1],
                 in_=wu_raw[b][:].rearrange("p (i m t) -> p m t i", i=PACK, t=PACK)[:, m0:m1],
             )
@@ -123,7 +122,8 @@ def tile_list_gmlpt_sigm_mix_resLP_kernel(
         def quantise_wu(b):
             nc.vector.quantize_mx(out=wu_w[b][:].bitcast(E4M3), scales=wu_s[b][:], in_=wu_bf[b][:])
 
-        round_wu(0, 0, P)
+        round_wu(0, 0, P - P // 4, nc.scalar.copy)
+        round_wu(0, P - P // 4, P, nc.vector.tensor_copy)
         quantise_wu(0)
 
         warm_sums = psum.tile([P, HALF], F32, name="ga", bufs=4)
@@ -135,12 +135,9 @@ def tile_list_gmlpt_sigm_mix_resLP_kernel(
                 start=(t == 0), stop=(t == PACK - 1),
             )
 
-        lists = [offsets[:, h * LIST_COLS : (h + 1) * LIST_COLS] for h in range(2)]
-        v_w = []
-        for h in range(2):
-            words = keep.tile([P, HALF], U32, name="v_w%d" % h, align_bytes=64)
-            nc.vector.tensor_copy(words[:], tab_w[:].bitcast(U32).indirect(lists[h]))
-            v_w.append(words)
+        v_w = keep.tile([P, J], U32, name="v_w", align_bytes=64)
+        for j0, j1 in ((0, QUARTER), (QUARTER, HALF), (HALF, J)):
+            nc.vector.tensor_copy(v_w[:, j0:j1], tab_w[:].bitcast(U32).indirect(offsets[:, j0 // 16 : j1 // 16]))
 
         wd4_w = keep.tile([P, 2 * N], U8, name="wd4_w", align_bytes=64)
 
@@ -153,7 +150,6 @@ def tile_list_gmlpt_sigm_mix_resLP_kernel(
 
         def gate_and_up(b, u, on_gpsimd):
             h, c0 = divmod(u * UNIT, HALF)
-            cols = slice(c0, c0 + UNIT)
             all_cols = slice(u * UNIT, (u + 1) * UNIT)
             ga = psum.tile([P, PACK, UNIT], F32, name="ga", bufs=4)
             for t in range(PACK):
@@ -162,7 +158,7 @@ def tile_list_gmlpt_sigm_mix_resLP_kernel(
                     out=ga[:, t, :],
                     lhsT=wg_w[:, 2 * w0 : 2 * (w0 + P)].bitcast(E2M1),
                     lhsT_scale=wg_s[:, w0 : w0 + P],
-                    rhs=v_w[h][:, cols].bitcast(E4M3),
+                    rhs=v_w[:, all_cols].bitcast(E4M3),
                     rhs_scale=v_s[:, all_cols],
                     start=True, stop=True,
                 )
@@ -175,7 +171,7 @@ def tile_list_gmlpt_sigm_mix_resLP_kernel(
                     out=ub[:, t, :],
                     lhsT=wu_w[b][:, t * P : (t + 1) * P].bitcast(E4M3),
                     lhsT_scale=wu_s[b][:, t * P : (t + 1) * P],
-                    rhs=v_w[h][:, cols].bitcast(E4M3),
+                    rhs=v_w[:, all_cols].bitcast(E4M3),
                     rhs_scale=v_s[:, all_cols],
                     start=True, stop=True,
                 )
@@ -203,9 +199,8 @@ def tile_list_gmlpt_sigm_mix_resLP_kernel(
         res = res_flat[:].rearrange("p (t j) -> p t j", t=PACK)
         y_sb = {
             (t, h): keep.tile([P, HALF], F32, name="y_sb%d%d" % (t, h), align_bytes=64)[:]
-            for h in range(2) for t in range(PACK) if (t, h) != (1, 0)
+            for h in range(2) for t in range(PACK)
         }
-        y_sb[1, 0] = res_flat[:, HALF:J]
 
         def down(t, h):
             y = psum.tile([P, HALF], F32, name="ga", bufs=4)

@@ -24,6 +24,8 @@ QUARTER = J // 4
 UNIT = 128
 STAGE = P - 16
 LAST = J - J // 8
+AHEAD = 1
+SHARE = P // 2
 
 
 def deal(nc, out, in_):
@@ -103,9 +105,6 @@ def tile_list_gmlpt_sigm_mix_resLP_kernel(
         nc.sync.dma_start(out=wd4_w_raw[:].bitcast(I32), in_=wd4_words[0].bitcast(I32))
         nc.sync.dma_start(out=r_win[0][:], in_=r_rows[:, 0, :])
 
-        wg_w = keep.tile([P, 2 * R], U8, name="wg_w", align_bytes=64)
-        deal(nc, wg_w[:].bitcast(U16), wg_w_raw[:].bitcast(U16))
-
         for t in range(1, PACK):
             nc.sync.dma_start(out=r_win[t][:], in_=r_rows[:, t, :])
 
@@ -122,9 +121,11 @@ def tile_list_gmlpt_sigm_mix_resLP_kernel(
         def quantise_wu(b):
             nc.vector.quantize_mx(out=wu_w[b][:].bitcast(E4M3), scales=wu_s[b][:], in_=wu_bf[b][:])
 
-        round_wu(0, 0, P - P // 4, nc.scalar.copy)
-        round_wu(0, P - P // 4, P, nc.vector.tensor_copy)
+        round_wu(0, 0, SHARE, nc.scalar.copy)
+        round_wu(0, SHARE, P, nc.vector.tensor_copy)
         quantise_wu(0)
+        wg_w = keep.tile([P, 2 * R], U8, name="wu_bf0", align_bytes=64)
+        deal(nc, wg_w[:].bitcast(U16), wg_w_raw[:].bitcast(U16))
 
         warm_sums = psum.tile([P, HALF], F32, name="ga", bufs=4)
         for t in range(PACK):
@@ -148,8 +149,9 @@ def tile_list_gmlpt_sigm_mix_resLP_kernel(
 
         h_bf = [h_regions[:, 3 * UNIT * PACK * h : 3 * UNIT * PACK * h + PACK * HALF] for h in range(2)]
 
-        def gate_and_up(b, u, on_gpsimd):
-            h, c0 = divmod(u * UNIT, HALF)
+        gates = {}
+
+        def gate_sums(b, u):
             all_cols = slice(u * UNIT, (u + 1) * UNIT)
             ga = psum.tile([P, PACK, UNIT], F32, name="ga", bufs=4)
             for t in range(PACK):
@@ -163,8 +165,16 @@ def tile_list_gmlpt_sigm_mix_resLP_kernel(
                     start=True, stop=True,
                 )
             gate_tile = ring.tile([P, UNIT * PACK], F32, name="gate", bufs=8)
+            nc.scalar.activation(
+                gate_tile[:].rearrange("p (j t) -> p j t", t=PACK), ga[:].rearrange("p t j -> p j t"), ACT.Sigmoid
+            )
+            gates[b, u] = gate_tile
+
+        def up_and_product(b, u, on_gpsimd):
+            h, c0 = divmod(u * UNIT, HALF)
+            all_cols = slice(u * UNIT, (u + 1) * UNIT)
+            gate_tile = gates[b, u]
             gate = gate_tile[:].rearrange("p (j t) -> p j t", t=PACK)
-            nc.scalar.activation(gate, ga[:].rearrange("p t j -> p j t"), ACT.Sigmoid)
             ub = psum.tile([P, PACK, UNIT], F32, name="ub", bufs=4)
             for t in range(PACK):
                 nc.tensor.matmul_mx(
@@ -224,24 +234,26 @@ def tile_list_gmlpt_sigm_mix_resLP_kernel(
             1.0, 0.0, ALU.mult, ALU.add,
         )
         wd8_w = keep.tile([P, N], I32, name="wu_raw1", align_bytes=64)
-        for u in range(4):
-            gate_and_up(0, u, False)
+        units = [(0, u, False) for u in range(4)]
         for b, h in ((0, 1), (1, 0), (1, 1)):
             shared = 3 + h
             own = [u for u in range(4 * h, 4 * h + 4) if u != shared]
-            gate_and_up(b, own[0], False)
-            if (b, h) == (0, 1):
+            units.extend([(b, own[0], False), (b, shared, True), (b, own[1], False), (b, own[2], False)])
+        for i in range(AHEAD):
+            gate_sums(*units[i][:2])
+        for i, unit in enumerate(units):
+            if i + AHEAD < len(units):
+                gate_sums(*units[i + AHEAD][:2])
+            up_and_product(*unit)
+            if i == 4:
                 deal_words(nc, wd8_w[:], wd8_w_raw[:])
                 quantise_wu(1)
                 quantise_h(0, 0)
-            elif (b, h) == (1, 0):
+            elif i == 8:
                 deal(nc, wd4_w[:].bitcast(U16), wd4_w_raw[:].bitcast(U16))
                 quantise_h(0, 1)
-            else:
+            elif i == 12:
                 quantise_h(1, 0)
-            gate_and_up(b, shared, True)
-            gate_and_up(b, own[1], False)
-            gate_and_up(b, own[2], False)
         for t in range(PACK):
             down(t, 0)
         quantise_h(1, 1)

@@ -25,7 +25,7 @@ UNIT = 128
 STAGE = P - 16
 LAST = J - J // 8
 AHEAD = 1
-SHARE = P // 2
+SHARE = P - P // 4
 
 
 def deal(nc, out, in_):
@@ -81,9 +81,9 @@ def tile_list_gmlpt_sigm_mix_resLP_kernel(
 
         nc.sync.dma_start(offsets[:], offs)
         nc.sync.dma_start(out=tab_s[STAGE:, :].bitcast(I32), in_=tab_scales[0].bitcast(I32))
-        nc.sync.dma_start(out=w_s_raw[STAGE:, :R].bitcast(I32), in_=wg_scales[0].bitcast(I32))
         nc.sync.dma_start(out=wg_w_raw[:].bitcast(I32), in_=wg_words[0].bitcast(I32))
         load_wu(0)
+        nc.sync.dma_start(out=w_s_raw[STAGE:, :R].bitcast(I32), in_=wg_scales[0].bitcast(I32))
         nc.sync.dma_start(out=w_s_raw[STAGE:, R : R + N].bitcast(I32), in_=wd8_scales[0].bitcast(I32))
         nc.sync.dma_start(out=w_s_raw[STAGE:, R + N :].bitcast(I32), in_=wd4_scales[0].bitcast(I32))
         nc.sync.dma_start(out=tab_w[:], in_=tab_words[0].rearrange("p t i -> p (t i)").bitcast(I32))
@@ -91,11 +91,10 @@ def tile_list_gmlpt_sigm_mix_resLP_kernel(
         nc.vector.tensor_copy(v_s_staged[:], tab_s[:].indirect(offsets[:]))
         first_s = keep.tile([P, R + J + 2 * N], U8, name="first_s", align_bytes=64)
         wg_s = first_s[:, :R]
-        v_s = first_s[:, R : R + J]
-        wd_s = first_s[:, R + J :]
-        deal(nc, wg_s, w_s_raw[:, :R])
+        wd_s = first_s[:, R : R + 2 * N]
+        v_s = first_s[:, R + 2 * N :]
         nc.vector.tensor_copy(v_s.bitcast(I32), v_s_staged[:].bitcast(I32))
-        deal(nc, wd_s, w_s_raw[:, R:])
+        deal(nc, first_s[:, : R + 2 * N], w_s_raw[:])
         for r in range(4):
             nc.sync.dma_start(
                 out=first_s[r:P:32, :].bitcast(I32), in_=first_s[STAGE + r : P : 4, :].bitcast(I32)
@@ -109,7 +108,7 @@ def tile_list_gmlpt_sigm_mix_resLP_kernel(
             nc.sync.dma_start(out=r_win[t][:], in_=r_rows[:, t, :])
 
         wu_bf = [keep.tile([P, PACK * PASS], BF16, name="wu_bf%d" % b, align_bytes=64) for b in range(2)]
-        wu_w = [keep.tile([P, PASS], U32, name="wu_w%d" % b, align_bytes=64) for b in range(2)]
+        wu_w = [keep.tile([P, PASS], U32, name=tag, align_bytes=64) for tag in ("w_s_raw", "wu_w1")]
         wu_s = [keep.tile([P, PASS], U8, name="wu_s%d" % b, align_bytes=64) for b in range(2)]
 
         def round_wu(b, m0, m1, copy):

@@ -81,11 +81,11 @@ def tile_list_gmlpt_sigm_mix_resLP_kernel(
 
         nc.sync.dma_start(offsets[:], offs)
         nc.sync.dma_start(out=tab_s[STAGE:, :].bitcast(I32), in_=tab_scales[0].bitcast(I32))
-        nc.sync.dma_start(out=wg_w_raw[:].bitcast(I32), in_=wg_words[0].bitcast(I32))
         load_wu(0)
         nc.sync.dma_start(out=w_s_raw[STAGE:, :R].bitcast(I32), in_=wg_scales[0].bitcast(I32))
         nc.sync.dma_start(out=w_s_raw[STAGE:, R : R + N].bitcast(I32), in_=wd8_scales[0].bitcast(I32))
         nc.sync.dma_start(out=w_s_raw[STAGE:, R + N :].bitcast(I32), in_=wd4_scales[0].bitcast(I32))
+        nc.sync.dma_start(out=wg_w_raw[:].bitcast(I32), in_=wg_words[0].bitcast(I32))
         nc.sync.dma_start(out=tab_w[:], in_=tab_words[0].rearrange("p t i -> p (t i)").bitcast(I32))
         v_s_staged = keep.tile([P, J], U8, name="v_s_staged", align_bytes=64)
         nc.vector.tensor_copy(v_s_staged[:], tab_s[:].indirect(offsets[:]))
@@ -208,8 +208,17 @@ def tile_list_gmlpt_sigm_mix_resLP_kernel(
         res = res_flat[:].rearrange("p (t j) -> p t j", t=PACK)
         y_sb = {
             (t, h): keep.tile([P, HALF], F32, name="y_sb%d%d" % (t, h), align_bytes=64)[:]
-            for h in range(2) for t in range(PACK)
+            for h in range(2) for t in range(PACK) if t != 2
         }
+        y_sb2 = keep.tile([P, J], F32, name="y_sb2", align_bytes=64)
+        for h in range(2):
+            y_sb[2, h] = y_sb2[:, h * HALF : (h + 1) * HALF]
+
+        def y_of(t, j0, j1):
+            if t == 2:
+                return y_sb2[:, j0:j1]
+            h = j0 // HALF
+            return y_sb[t, h][:, j0 - h * HALF : j1 - h * HALF]
 
         def down(t, h):
             y = psum.tile([P, HALF], F32, name="ga", bufs=4)
@@ -263,10 +272,8 @@ def tile_list_gmlpt_sigm_mix_resLP_kernel(
         words_out = out_1[0].rearrange("p j i -> p (j i)").bitcast(I32)
         o_s = keep.tile([P, J], U8, name="o_s", align_bytes=64)
         def add_residual(t, j0, j1):
-            h = j0 // HALF
             nc.vector.tensor_tensor(
-                res[:, t, j0:j1], r_win[t][:].indirect(offsets[:, j0 // 16 : j1 // 16]),
-                y_sb[t, h][:, j0 - h * HALF : j1 - h * HALF], ALU.add,
+                res[:, t, j0:j1], r_win[t][:].indirect(offsets[:, j0 // 16 : j1 // 16]), y_of(t, j0, j1), ALU.add
             )
 
         def store_result(t0, t1, j0, j1):
@@ -300,8 +307,7 @@ def tile_list_gmlpt_sigm_mix_resLP_kernel(
         add_residual(1, HALF, J)
         round_pair(0, HALF, J, nc.scalar.copy)
         store_result(0, 2, 0, J)
-        add_residual(2, 0, HALF)
-        add_residual(2, HALF, J)
+        add_residual(2, 0, J)
         store_result(2, 3, 0, J)
         for j0 in range(0, J, QUARTER):
             add_residual(3, j0, j0 + QUARTER)

@@ -25,6 +25,7 @@ UNIT = 128
 STAGE = P - 16
 LAST = J - J // 8
 AHEAD = 1
+OUT_ROW = 12
 SHARE = P - P // 4
 
 
@@ -294,7 +295,7 @@ def tile_list_gmlpt_sigm_mix_resLP_kernel(
 
         def quantise_out(j0, j1):
             nc.vector.quantize_mx(
-                out=o_w[:, j0:j1].bitcast(E4M3), scales=o_s[:, j0:j1],
+                out=o_w[:, j0:j1].bitcast(E4M3), scales=o_s[OUT_ROW:, j0:j1],
                 in_=rounded(j0, j1),
             )
 
@@ -309,11 +310,12 @@ def tile_list_gmlpt_sigm_mix_resLP_kernel(
         store_result(0, 2, 0, J)
         add_residual(2, 0, J)
         store_result(2, 3, 0, J)
-        for j0 in range(0, J, QUARTER):
-            add_residual(3, j0, j0 + QUARTER)
-            round_pair(2, j0, min(j0 + QUARTER, LAST), nc.scalar.copy)
-            if j0 % HALF:
-                store_result(3, 4, j0 - QUARTER, j0 + QUARTER)
+        cuts = [0, J // 8, QUARTER, HALF, HALF + QUARTER, J]
+        for j0, j1 in zip(cuts, cuts[1:]):
+            add_residual(3, j0, j1)
+            round_pair(2, j0, min(j1, LAST), nc.scalar.copy)
+            if j1 % HALF == 0:
+                store_result(3, 4, j1 - HALF, j1)
         for j0, j1 in ((0, 512), (512, 768), (768, 1024)):
             quantise_out(j0, j1)
             if j0 == 0:
@@ -323,5 +325,5 @@ def tile_list_gmlpt_sigm_mix_resLP_kernel(
             queue = nc.scalar if q % 2 else nc.sync
             queue.dma_start(
                 out=out_2[0, q:16:4, :].bitcast(I32),
-                in_=o_s[q:P:32, :].bitcast(I32),
+                in_=o_s[OUT_ROW + q : P : 32, :].bitcast(I32),
             )

@@ -197,13 +197,14 @@ def tile_list_gmlpt_sigm_mix_resLP_kernel(
                     h_unit.rearrange("p (j t) -> p j t", t=PACK), ub[:].rearrange("p t j -> p j t"), gate, ALU.mult
                 )
 
-        def quantise_h(b, h):
+        def quantise_h(b, h, pieces=((0, HALF),)):
             h_w[b, h] = keep.tile([P, HALF], U32, name="h_w%d%d" % (b, h), align_bytes=64)
             h_s[b, h] = keep.tile([P, HALF], U8, name="h_s%d%d" % (b, h), align_bytes=64)
-            nc.vector.quantize_mx(
-                out=h_w[b, h][:].bitcast(E4M3), scales=h_s[b, h][:],
-                in_=h_bf[h],
-            )
+            for c0, c1 in pieces:
+                nc.vector.quantize_mx(
+                    out=h_w[b, h][:, c0:c1].bitcast(E4M3), scales=h_s[b, h][:, c0:c1],
+                    in_=h_bf[h][:, PACK * c0 : PACK * c1],
+                )
 
         res_flat = keep.tile([P, PACK * J], F32, name="res")
         res = res_flat[:].rearrange("p (t j) -> p t j", t=PACK)
@@ -247,6 +248,8 @@ def tile_list_gmlpt_sigm_mix_resLP_kernel(
         for b, h in ((0, 1), (1, 0), (1, 1)):
             shared = 3 + h
             own = [u for u in range(4 * h, 4 * h + 4) if u != shared]
+            if b + h == 2:
+                own.reverse()
             units.extend([(b, own[0], False), (b, shared, True), (b, own[1], False), (b, own[2], False)])
         for i in range(AHEAD):
             gate_sums(*units[i][:2])
@@ -265,7 +268,7 @@ def tile_list_gmlpt_sigm_mix_resLP_kernel(
                 quantise_h(1, 0)
         for t in range(PACK):
             down(t, 0)
-        quantise_h(1, 1)
+        quantise_h(1, 1, ((QUARTER, HALF), (0, QUARTER)))
         for t in range(PACK):
             down(t, 1)
 

from contextlib import ExitStack

import concourse.mybir as mybir

K, R, N, T, J = 512, 1024, 512, 4096, 1024
FLOPS = 2 * K * R * J * 2 + 2 * R * N * J

F32 = mybir.dt.float32
BF16 = mybir.dt.bfloat16
I32 = mybir.dt.int32
U32 = mybir.dt.uint32
U16 = mybir.dt.uint16
U8 = mybir.dt.uint8
E4M3 = mybir.dt.float8_e4m3fn_x4
E2M1 = mybir.dt.float4_e2m1fn_x4
ACT = mybir.ActivationFunctionType
ALU = mybir.AluOpType

P = 128
PACK = 4
PASS = P * PACK
HALF = J // 2
QUARTER = J // 4
UNIT = 128
STAGE = P - 16
LAST = J - J // 8
AHEAD = 1
OUT_ROW = 12
SHARE = P - P // 4


def deal(nc, out, in_):
    nc.vector.tensor_copy(
        out=out.rearrange("p (b t m) -> p b t m", t=PACK, m=P),
        in_=in_.rearrange("p (b m t) -> p b t m", t=PACK, m=P),
    )


def deal_words(nc, out, in_):
    nc.vector.tensor_copy(
        out=out.rearrange("p (t c i) -> p c t i", t=PACK, i=4),
        in_=in_.rearrange("p (c i t) -> p c t i", t=PACK, i=4),
    )


def tile_list_gmlpt_sigm_mix_resLP_kernel(
    tc, tab_words, tab_scales, wg_words, wg_scales, wu, wd8_words, wd8_scales,
    wd4_words, wd4_scales, rT, offs, out_0, out_1, out_2,
):
    nc = tc.nc
    with ExitStack() as ctx:
        keep = ctx.enter_context(tc.tile_pool(name="keep", bufs=1))
        ring = ctx.enter_context(tc.tile_pool(name="ring", bufs=2))
        psum = ctx.enter_context(tc.psum_pool(name="psum", bufs=1))

        offsets = keep.tile([P, J // 16], U16, name="offsets")
        tab_w = keep.tile([P, T], I32, name="tab_w", align_bytes=64)
        tab_s = keep.tile([P, T], U8, name="tab_s", align_bytes=64)
        wg_w_raw = keep.tile([P, 2 * R], U8, name="wg_w_raw", align_bytes=64)
        wd8_w_raw = keep.tile([P, N], I32, name="wd8_w_raw", align_bytes=64)
        wd4_w_raw = keep.tile([P, 2 * N], U8, name="wd4_w_raw", align_bytes=64)
        w_s_raw = keep.tile([P, R + 2 * N], U8, name="w_s_raw", align_bytes=64)
        warm = keep.tile([P, 8], F32, name="warm")
        warm_out = keep.tile([P, 8], F32, name="warm_out")

        nc.vector.memset(warm[:], 0.0)
        nc.vector.memset(tab_s[:STAGE, :].bitcast(I32), 0)
        nc.vector.memset(w_s_raw[:STAGE, :].bitcast(I32), 0)
        nc.scalar.activation(warm_out[:], warm[:], ACT.Sigmoid)

        wu_rows = wu.rearrange("(p i) r -> p i r", i=PACK)
        wu_raw = [keep.tile([P, PACK * PASS], F32, name="wu_raw%d" % b, align_bytes=64) for b in range(2)]

        def load_wu(b):
            nc.sync.dma_start(
                out=wu_raw[b][:].rearrange("p (i c) -> p i c", i=PACK),
                in_=wu_rows[:, :, b * PASS : (b + 1) * PASS],
            )

        r_rows = rT.rearrange("(p t) c -> p t c", t=PACK)
        r_win = [keep.tile([P, T], F32, name="r_win%d" % t) for t in range(PACK)]

        nc.sync.dma_start(offsets[:], offs)
        nc.sync.dma_start(out=tab_s[STAGE:, :].bitcast(I32), in_=tab_scales[0].bitcast(I32))
        load_wu(0)
        nc.sync.dma_start(out=w_s_raw[STAGE:, :R].bitcast(I32), in_=wg_scales[0].bitcast(I32))
        nc.sync.dma_start(out=w_s_raw[STAGE:, R : R + N].bitcast(I32), in_=wd8_scales[0].bitcast(I32))
        nc.sync.dma_start(out=w_s_raw[STAGE:, R + N :].bitcast(I32), in_=wd4_scales[0].bitcast(I32))
        nc.sync.dma_start(out=wg_w_raw[:].bitcast(I32), in_=wg_words[0].bitcast(I32))
        nc.sync.dma_start(out=tab_w[:], in_=tab_words[0].rearrange("p t i -> p (t i)").bitcast(I32))
        v_s_staged = keep.tile([P, J], U8, name="v_s_staged", align_bytes=64)
        nc.vector.tensor_copy(v_s_staged[:], tab_s[:].indirect(offsets[:]))
        first_s = keep.tile([P, R + J + 2 * N], U8, name="first_s", align_bytes=64)
        wg_s = first_s[:, :R]
        wd_s = first_s[:, R : R + 2 * N]
        v_s = first_s[:, R + 2 * N :]
        nc.vector.tensor_copy(v_s.bitcast(I32), v_s_staged[:].bitcast(I32))
        deal(nc, first_s[:, : R + 2 * N], w_s_raw[:])
        for r in range(4):
            nc.sync.dma_start(
                out=first_s[r:P:32, :].bitcast(I32), in_=first_s[STAGE + r : P : 4, :].bitcast(I32)
            )
        load_wu(1)
        nc.sync.dma_start(out=wd8_w_raw[:], in_=wd8_words[0].rearrange("p n i -> p (n i)").bitcast(I32))
        nc.sync.dma_start(out=wd4_w_raw[:].bitcast(I32), in_=wd4_words[0].bitcast(I32))
        nc.sync.dma_start(out=r_win[0][:], in_=r_rows[:, 0, :])

        for t in range(1, PACK):
            nc.sync.dma_start(out=r_win[t][:], in_=r_rows[:, t, :])

        wu_bf = [keep.tile([P, PACK * PASS], BF16, name="wu_bf%d" % b, align_bytes=64) for b in range(2)]
        wu_w = [keep.tile([P, PASS], U32, name=tag, align_bytes=64) for tag in ("w_s_raw", "wu_w1")]
        wu_s = [keep.tile([P, PASS], U8, name="wu_s%d" % b, align_bytes=64) for b in range(2)]

        def round_wu(b, m0, m1, copy):
            copy(
                out=wu_bf[b][:].rearrange("p (t m i) -> p m t i", t=PACK, i=PACK)[:, m0:m1],
                in_=wu_raw[b][:].rearrange("p (i m t) -> p m t i", i=PACK, t=PACK)[:, m0:m1],
            )

        def quantise_wu(b):
            nc.vector.quantize_mx(out=wu_w[b][:].bitcast(E4M3), scales=wu_s[b][:], in_=wu_bf[b][:])

        round_wu(0, 0, SHARE, nc.scalar.copy)
        round_wu(0, SHARE, P, nc.vector.tensor_copy)
        quantise_wu(0)
        wg_w = keep.tile([P, 2 * R], U8, name="wu_bf0", align_bytes=64)
        deal(nc, wg_w[:].bitcast(U16), wg_w_raw[:].bitcast(U16))

        warm_sums = psum.tile([P, HALF], F32, name="ga", bufs=4)
        for t in range(PACK):
            nc.tensor.matmul_mx(
                out=warm_sums[:], lhsT=wu_w[0][:, t * P : (t + 1) * P].bitcast(E4M3),
                lhsT_scale=wu_s[0][:, t * P : (t + 1) * P],
                rhs=wu_w[0][:].bitcast(E4M3), rhs_scale=wu_s[0][:],
                start=(t == 0), stop=(t == PACK - 1),
            )

        v_w = keep.tile([P, J], U32, name="v_w", align_bytes=64)
        for j0, j1 in ((0, QUARTER), (QUARTER, HALF), (HALF, J)):
            nc.vector.tensor_copy(v_w[:, j0:j1], tab_w[:].bitcast(U32).indirect(offsets[:, j0 // 16 : j1 // 16]))

        wd4_w = keep.tile([P, 2 * N], U8, name="wd4_w", align_bytes=64)

        h_w = {}
        h_s = {}

        h_regions = keep.tile([P, 7 * UNIT * PACK], BF16, name="h_regions", align_bytes=64)

        h_bf = [h_regions[:, 3 * UNIT * PACK * h : 3 * UNIT * PACK * h + PACK * HALF] for h in range(2)]

        gates = {}

        def gate_sums(b, u):
            all_cols = slice(u * UNIT, (u + 1) * UNIT)
            ga = psum.tile([P, PACK, UNIT], F32, name="ga", bufs=4)
            for t in range(PACK):
                w0 = b * PASS + t * P
                nc.tensor.matmul_mx(
                    out=ga[:, t, :],
                    lhsT=wg_w[:, 2 * w0 : 2 * (w0 + P)].bitcast(E2M1),
                    lhsT_scale=wg_s[:, w0 : w0 + P],
                    rhs=v_w[:, all_cols].bitcast(E4M3),
                    rhs_scale=v_s[:, all_cols],
                    start=True, stop=True,
                )
            gate_tile = ring.tile([P, UNIT * PACK], F32, name="gate", bufs=8)
            nc.scalar.activation(
                gate_tile[:].rearrange("p (j t) -> p j t", t=PACK), ga[:].rearrange("p t j -> p j t"), ACT.Sigmoid
            )
            gates[b, u] = gate_tile

        def up_and_product(b, u, on_gpsimd):
            h, c0 = divmod(u * UNIT, HALF)
            all_cols = slice(u * UNIT, (u + 1) * UNIT)
            gate_tile = gates[b, u]
            gate = gate_tile[:].rearrange("p (j t) -> p j t", t=PACK)
            ub = psum.tile([P, PACK, UNIT], F32, name="ub", bufs=4)
            for t in range(PACK):
                nc.tensor.matmul_mx(
                    out=ub[:, t, :],
                    lhsT=wu_w[b][:, t * P : (t + 1) * P].bitcast(E4M3),
                    lhsT_scale=wu_s[b][:, t * P : (t + 1) * P],
                    rhs=v_w[:, all_cols].bitcast(E4M3),
                    rhs_scale=v_s[:, all_cols],
                    start=True, stop=True,
                )
            h_unit = h_bf[h][:, PACK * c0 : PACK * (c0 + UNIT)]
            if on_gpsimd:
                up_tile = ring.tile([P, UNIT * PACK], F32, name="up")
                nc.scalar.copy(
                    out=up_tile[:].rearrange("p (j t) -> p j t", t=PACK), in_=ub[:].rearrange("p t j -> p j t")
                )
                nc.gpsimd.tensor_tensor(h_unit, up_tile[:], gate_tile[:], ALU.mult)
            else:
                nc.vector.tensor_tensor(
                    h_unit.rearrange("p (j t) -> p j t", t=PACK), ub[:].rearrange("p t j -> p j t"), gate, ALU.mult
                )

        def quantise_h(b, h, pieces=((0, HALF),)):
            h_w[b, h] = keep.tile([P, HALF], U32, name="h_w%d%d" % (b, h), align_bytes=64)
            h_s[b, h] = keep.tile([P, HALF], U8, name="h_s%d%d" % (b, h), align_bytes=64)
            for c0, c1 in pieces:
                nc.vector.quantize_mx(
                    out=h_w[b, h][:, c0:c1].bitcast(E4M3), scales=h_s[b, h][:, c0:c1],
                    in_=h_bf[h][:, PACK * c0 : PACK * c1],
                )

        res_flat = keep.tile([P, PACK * J], F32, name="res")
        res = res_flat[:].rearrange("p (t j) -> p t j", t=PACK)
        y_sb = {
            (t, h): keep.tile([P, HALF], F32, name="y_sb%d%d" % (t, h), align_bytes=64)[:]
            for h in range(2) for t in range(PACK) if t != 2
        }
        y_sb2 = keep.tile([P, J], F32, name="y_sb2", align_bytes=64)
        for h in range(2):
            y_sb[2, h] = y_sb2[:, h * HALF : (h + 1) * HALF]

        def y_of(t, j0, j1):
            if t == 2:
                return y_sb2[:, j0:j1]
            h = j0 // HALF
            return y_sb[t, h][:, j0 - h * HALF : j1 - h * HALF]

        def down(t, h):
            y = psum.tile([P, HALF], F32, name="ga", bufs=4)
            nc.tensor.matmul_mx(
                out=y[:], lhsT=wd8_w[:, t * P : (t + 1) * P].bitcast(E4M3),
                lhsT_scale=wd_s[:, t * P : (t + 1) * P],
                rhs=h_w[0, h][:].bitcast(E4M3), rhs_scale=h_s[0, h][:],
                start=True, stop=False,
            )
            nc.tensor.matmul_mx(
                out=y[:], lhsT=wd4_w[:, 2 * t * P : 2 * (t + 1) * P].bitcast(E2M1),
                lhsT_scale=wd_s[:, N + t * P : N + (t + 1) * P],
                rhs=h_w[1, h][:].bitcast(E4M3), rhs_scale=h_s[1, h][:],
                start=False, stop=True,
            )
            nc.scalar.copy(out=y_sb[t, h], in_=y[:])

        nc.gpsimd.tensor_scalar(
            wu_bf[1][:].rearrange("p (t m i) -> p m t i", t=PACK, i=PACK),
            wu_raw[1][:].rearrange("p (i m t) -> p m t i", i=PACK, t=PACK),
            1.0, 0.0, ALU.mult, ALU.add,
        )
        wd8_w = keep.tile([P, N], I32, name="wu_raw1", align_bytes=64)
        units = [(0, u, False) for u in range(4)]
        for b, h in ((0, 1), (1, 0), (1, 1)):
            shared = 3 + h
            own = [u for u in range(4 * h, 4 * h + 4) if u != shared]
            if b + h == 2:
                own.reverse()
            units.extend([(b, own[0], False), (b, shared, True), (b, own[1], False), (b, own[2], False)])
        for i in range(AHEAD):
            gate_sums(*units[i][:2])
        for i, unit in enumerate(units):
            if i + AHEAD < len(units):
                gate_sums(*units[i + AHEAD][:2])
            up_and_product(*unit)
            if i == 4:
                deal_words(nc, wd8_w[:], wd8_w_raw[:])
                quantise_wu(1)
                quantise_h(0, 0)
            elif i == 8:
                deal(nc, wd4_w[:].bitcast(U16), wd4_w_raw[:].bitcast(U16))
                quantise_h(0, 1)
            elif i == 12:
                quantise_h(1, 0)
        for t in range(PACK):
            down(t, 0)
        quantise_h(1, 1, ((QUARTER, HALF), (0, QUARTER)))
        for t in range(PACK):
            down(t, 1)

        out_rows = out_0.rearrange("(p t) j -> p t j", t=PACK)
        words_out = out_1[0].rearrange("p j i -> p (j i)").bitcast(I32)
        o_s = keep.tile([P, J], U8, name="o_s", align_bytes=64)
        def add_residual(t, j0, j1):
            nc.vector.tensor_tensor(
                res[:, t, j0:j1], r_win[t][:].indirect(offsets[:, j0 // 16 : j1 // 16]), y_of(t, j0, j1), ALU.add
            )

        def store_result(t0, t1, j0, j1):
            nc.sync.dma_start(out=out_rows[:, t0:t1, j0:j1], in_=res[:, t0:t1, j0:j1])

        res_bf = {}
        o_w = keep.tile([P, J], I32, name="o_w", align_bytes=64)

        def rounded(j0, j1):
            h = j0 // HALF
            return res_bf[h][:, PACK * (j0 - h * HALF) : PACK * (j1 - h * HALF)]

        def round_pair(t0, j0, j1, copy):
            copy(
                out=rounded(j0, j1).rearrange("p (c i t) -> p c t i", i=2, t=PACK)[:, :, t0 : t0 + 2],
                in_=res[:, t0 : t0 + 2, j0:j1].rearrange("p t (c i) -> p c t i", i=2),
            )

        def quantise_out(j0, j1):
            nc.vector.quantize_mx(
                out=o_w[:, j0:j1].bitcast(E4M3), scales=o_s[OUT_ROW:, j0:j1],
                in_=rounded(j0, j1),
            )

        for t in range(2):
            add_residual(t, 0, HALF)
        add_residual(0, HALF, J)
        res_bf[0] = keep.tile([P, HALF * PACK], BF16, name="y_sb01", align_bytes=64)
        res_bf[1] = keep.tile([P, HALF * PACK], BF16, name="res_bf1", align_bytes=64)
        round_pair(0, 0, HALF, nc.scalar.copy)
        add_residual(1, HALF, J)
        round_pair(0, HALF, J, nc.scalar.copy)
        store_result(0, 2, 0, J)
        add_residual(2, 0, J)
        store_result(2, 3, 0, J)
        cuts = [0, J // 8, QUARTER, HALF, HALF + QUARTER, J]
        for j0, j1 in zip(cuts, cuts[1:]):
            add_residual(3, j0, j1)
            round_pair(2, j0, min(j1, LAST), nc.scalar.copy)
            if j1 % HALF == 0:
                store_result(3, 4, j1 - HALF, j1)
        for j0, j1 in ((0, 512), (512, 768), (768, 1024)):
            quantise_out(j0, j1)
            if j0 == 0:
                round_pair(2, LAST, J, nc.vector.tensor_copy)
            nc.sync.dma_start(out=words_out[:, j0:j1], in_=o_w[:, j0:j1])
        for q in range(4):
            queue = nc.scalar if q % 2 else nc.sync
            queue.dma_start(
                out=out_2[0, q:16:4, :].bitcast(I32),
                in_=o_s[OUT_ROW + q : P : 32, :].bitcast(I32),
            )
